import numpy as np
import ml_dtypes


def mxq(x, axis, fmt="e4m3"):
    dtype, down = {"e4m3": (ml_dtypes.float8_e4m3fn, 7), "e5m2": (ml_dtypes.float8_e5m2, 14)}[fmt]
    v = np.moveaxis(np.asarray(x, np.float32).astype(ml_dtypes.bfloat16).astype(np.float64), axis, -1)
    blocks = v.reshape(v.shape[:-1] + (-1, 32))
    amax = np.abs(blocks).max(-1, keepdims=True)
    byte = np.maximum(np.where(amax > 0, np.frexp(amax)[1] - 1 + 127, 0) - down, 1)
    scale = np.exp2(byte - 127.0)
    codes = (blocks / scale).astype(np.float32).astype(dtype).astype(np.float64)
    return np.moveaxis((codes * scale).reshape(v.shape), -1, axis)


WIDE = False


def mx_kscale(k):
    if not WIDE:
        return np.ones(k)
    levels = np.array([10, -10, 5, -5, 0])
    if k % 512:
        return np.exp2(np.random.permutation(np.resize(levels, k // 32))).repeat(32)
    a = np.empty((k // 512, 16))
    for p in range(k // 512):
        a[p, :8] = np.random.permutation(np.resize(levels, 8))
        for g in range(8):
            far = levels[np.abs(levels - a[p, g]) >= 10]
            a[p, g + 8] = far[np.random.randint(len(far))]
    return np.exp2(a.ravel()).repeat(32)


BF16 = ml_dtypes.bfloat16


def bf(x):
    return np.asarray(x, np.float32).astype(BF16)


def f64(x):
    return np.asarray(x).astype(np.float64)

def planes(Y):
    n, m = Y.shape
    b = f64(bf(Y)).reshape(n // 32, 32, m)
    amax = np.abs(b).max(1)
    byte = np.clip(np.where(amax > 0, np.frexp(amax)[1] - 1 + 127 - 7, 1), 1, 254)
    codes = (b * np.exp2(127.0 - byte)[:, None, :]).reshape(n, m).astype(np.float32).astype(ml_dtypes.float8_e4m3fn).view(np.uint8)
    words = codes.reshape(n // 512, 128, 4, m).transpose(0, 1, 3, 2)
    return np.ascontiguousarray(words), np.ascontiguousarray(byte.astype(np.uint8).reshape(n // 512, 16, m))


E, S, D, R = 4, 512, 2048, 512


def setup_inputs():
    s = mx_kscale(D)
    x = np.random.randn(E, S, D) * s
    a_down = np.random.randn(E, R, D) / np.sqrt(D) / s
    gain = np.exp(0.8 * np.random.randn(E, R))
    alpha = 1.5 * R * np.exp(0.3 * np.random.randn(E))
    return {"x": bf(x), "a_down": bf(a_down), "gain": bf(gain), "alpha": bf(alpha)}


def reference(x, a_down, gain, alpha):
    xq = mxq(f64(x), 2, "e4m3")
    aq = mxq(f64(a_down), 2, "e4m3")
    h = aq @ xq.swapaxes(1, 2)
    y = h * f64(gain)[:, :, None] * (f64(alpha) / R)[:, None, None]
    Y = y.transpose(1, 0, 2).reshape(R, E * S)
    words, scales = planes(Y)
    return y, words, scales

@@ -1,0 +1,327 @@
+from contextlib import ExitStack
+
+import concourse.mybir as mybir
+from concourse.masks import make_identity
+
+E, S, D, R = 4, 512, 2048, 512
+FLOPS = 2 * E * S * D * R
+
+F32 = mybir.dt.float32
+BF16 = mybir.dt.bfloat16
+U32 = mybir.dt.uint32
+I32 = mybir.dt.int32
+U8 = mybir.dt.uint8
+FP8X4 = mybir.dt.float8_e4m3fn_x4
+MULT = mybir.AluOpType.mult
+COPY = mybir.ActivationFunctionType.Copy
+
+P = 128
+PASSES = 4
+RAW_BUFS = 12
+T_BANKS = 6
+FIRST_MM_STEP = 2
+A_FIRST = 1
+BY_TILE = (1, 2)
+FACTOR_STEP = 1
+HEAD = 3
+VORD_H = "qa s0 g0 qb qc s1 g1 e o qd"
+VORD = "s0 qa g0 s1 o g1 qb qc e qd"
+QLAG_H = 1
+MM_AFTER = [m + 2 for m in range(14)]
+SPLIT_Q = (15,)
+QY = 1
+TAILQ = 1
+V_BANKS = ((3, 3), (7, 3), (11, 3), (15, 3))
+AHEAD_FROM = 99
+QLAG = 1
+VORD_X = "s0 qa g0 s1 qb g1 e o qc qd"
+VORD_A = "s0 qa g0 s1 qb g1 e o qc qd"
+ACC_POS = 0
+SINGLE = 3
+
+
+def tile_lora_down_scaled_rank_planes_g2_kernel(tc, x, a_down, gain, alpha, out_0, out_1, out_2):
+    nc = tc.nc
+    steps = []
+    for e in range(E):
+        steps += [("a", e, 0), ("x", e, 0), ("x", e, 1), ("a", e, 1)] if e < A_FIRST else [("x", e, 0), ("a", e, 0), ("x", e, 1), ("a", e, 1)]
+    words_out = out_1[0].rearrange("p m t -> p (m t)").bitcast(I32)
+
+    with ExitStack() as ctx:
+        keep = ctx.enter_context(tc.tile_pool(name="keep", bufs=1))
+        work = ctx.enter_context(tc.tile_pool(name="work", bufs=2))
+        psum = ctx.enter_context(tc.psum_pool(name="psum", bufs=2))
+        ctx.enter_context(tc.manual_schedule())
+
+        ident = keep.tile([P, P], F32, name="ident")
+        gain_sb = keep.tile([P, E, 4], BF16, name="gain_sb")
+        alpha_sb = keep.tile([P, E], BF16, name="alpha_sb")
+        factor = keep.tile([P, E, 4], F32, name="factor")
+        warm = keep.tile([P, 1], F32, name="warm")
+        y_codes = keep.tile([P, E * S], U32, name="y_codes", align_bytes=64)
+        y_scales = keep.tile([P, E * S], U8, name="y_scales", align_bytes=64)
+
+        raw, second, banks, grouped = {}, {}, {}, {}
+        x_codes, x_scales, a_codes, a_scales, acc, y32, y16 = {}, {}, {}, {}, {}, {}, {}
+
+        def load(s):
+            kind, e, h = steps[s]
+            raw[s] = work.tile([P, 2, D], BF16, name="raw", bufs=RAW_BUFS, align_bytes=64)
+            if kind == "x":
+                src = x[e, 256 * h : 256 * (h + 1), :].rearrange("(j p) k -> p j k", p=P)
+            else:
+                src = a_down[e].rearrange("(p t) k -> p t k", t=4)[:, 2 * h : 2 * h + 2, :]
+            if s < SINGLE:
+                for j in range(2):
+                    nc.sync.dma_start(out=raw[s][:, j, :], in_=src[:, j, :])
+            else:
+                nc.sync.dma_start(out=raw[s][:], in_=src)
+
+        def halves(s, j):
+            return raw[s][:, j, :].rearrange("p (h b u i) -> p h b u i", h=2, u=2, i=16)
+
+        def save_second(s, j):
+            if s >= len(steps):
+                return
+            second[s, j] = work.tile([P, D // 2], BF16, name="second", bufs=6, align_bytes=64)
+            nc.vector.tensor_copy(
+                out=second[s, j][:].rearrange("p (b h i) -> p h b i", h=2, i=16),
+                in_=halves(s, j)[:, :, :, 1, :],
+            )
+
+        def gather_first(s, j):
+            if s >= len(steps):
+                return
+            nc.vector.tensor_copy(out=halves(s, j)[:, 0, :, 1, :], in_=halves(s, j)[:, 1, :, 0, :])
+
+        def bank_items(s, b):
+            if steps[s][0] == "x" and s not in BY_TILE:
+                return [(0, b), (1, b)]
+            return [(b // 2, 2 * (b % 2)), (b // 2, 2 * (b % 2) + 1)]
+
+        def transposes(s, b):
+            banks[s, b] = psum.tile([P, 2, 2, P], F32, name="bank", bufs=T_BANKS)
+            for n, (j, g) in enumerate(bank_items(s, b)):
+                first_words = raw[s][:, j, : D // 2].bitcast(F32)
+                second_words = second[s, j][:].bitcast(F32)
+                for u, words in enumerate((first_words, second_words)):
+                    nc.tensor.transpose(banks[s, b][:, n, u, :], words[:, P * g : P * (g + 1)], ident[:])
+
+        def empty_bank(s, b):
+            if b % 2 == 0:
+                grouped[s, b // 2] = work.tile([P, 2, 4 * 2 * P], BF16, name="grouped", bufs=4, align_bytes=64)
+            dst = grouped[s, b // 2][:, b % 2, :].bitcast(F32).rearrange("p (n r u) -> p n r u", n=2, u=2)
+            src = banks[s, b][:].rearrange("p n u r -> p n r u")
+            if (s, b) in V_BANKS:
+                nc.vector.tensor_copy(out=dst, in_=src)
+            else:
+                nc.scalar.copy(out=dst, in_=src)
+
+        def quantise(s, b):
+            kind, e, h = steps[s]
+            if kind == "x":
+                if h == 0 and b == 0:
+                    x_codes[e] = work.tile([P, PASSES, S], U32, name="x_codes", align_bytes=64)
+                    x_scales[e] = work.tile([P, PASSES, S], U8, name="x_scales", align_bytes=64)
+                if s in BY_TILE:
+                    for n, (j, g) in enumerate(bank_items(s, b)):
+                        cols = slice(256 * h + P * j, 256 * h + P * (j + 1))
+                        nc.vector.quantize_mx(
+                            out=x_codes[e][:, g, cols].bitcast(FP8X4),
+                            scales=x_scales[e][:, g, cols],
+                            in_=grouped[s, b // 2][:, b % 2, 4 * P * n : 4 * P * (n + 1)],
+                        )
+                    return
+                cols = slice(256 * h, 256 * (h + 1))
+                nc.vector.quantize_mx(
+                    out=x_codes[e][:, b, cols].bitcast(FP8X4),
+                    scales=x_scales[e][:, b, cols],
+                    in_=grouped[s, b // 2][:, b % 2, :],
+                )
+                return
+            t = 2 * h + b // 2
+            if b % 2 == (0 if s in SPLIT_Q else 1):
+                a_codes[e, t] = work.tile([P, PASSES * P], U32, name="a_codes", bufs=5, align_bytes=64)
+                a_scales[e, t] = work.tile([P, PASSES * P], U8, name="a_scales", bufs=5, align_bytes=64)
+            if s in SPLIT_Q:
+                cols = slice(256 * (b % 2), 256 * (b % 2 + 1))
+                nc.vector.quantize_mx(
+                    out=a_codes[e, t][:, cols].bitcast(FP8X4),
+                    scales=a_scales[e, t][:, cols],
+                    in_=grouped[s, b // 2][:, b % 2, :],
+                )
+            elif b % 2 == 1:
+                nc.vector.quantize_mx(
+                    out=a_codes[e, t][:].bitcast(FP8X4),
+                    scales=a_scales[e, t][:],
+                    in_=grouped[s, b // 2][:].rearrange("p n c -> p (n c)"),
+                )
+
+        def group_items(m):
+            e, n = divmod(m, 4)
+            if n < 2:
+                return [(e, t, slice(256 * n, 256 * (n + 1))) for t in range(2)]
+            return [(e, n, slice(0, S))]
+
+        def multiply(key, items, tag="acc"):
+            acc[key] = psum.tile([P, S], F32, name=tag, bufs=8 - T_BANKS if tag == "acc" else T_BANKS)
+            at = 0
+            for e, t, cols in items:
+                width = cols.stop - cols.start
+                for g in range(PASSES):
+                    nc.tensor.matmul_mx(
+                        out=acc[key][:, at : at + width],
+                        lhsT=a_codes[e, t][:, P * g : P * (g + 1)].bitcast(FP8X4),
+                        lhsT_scale=a_scales[e, t][:, P * g : P * (g + 1)],
+                        rhs=x_codes[e][:, g, cols].bitcast(FP8X4),
+                        rhs_scale=x_scales[e][:, g, cols],
+                        start=(g == 0),
+                        stop=(g == PASSES - 1),
+                    )
+                at += width
+
+        def scale_out(key, items):
+            at = 0
+            for e, t, cols in items:
+                width = cols.stop - cols.start
+                if e not in y32:
+                    y32[e] = work.tile([P, 4, S], F32, name="y32", bufs=E)
+                nc.scalar.activation(
+                    out=y32[e][:, t, cols], in_=acc[key][:, at : at + width], func=COPY, scale=factor[:, e, t : t + 1]
+                )
+                at += width
+
+        def round_y(e, cols):
+            if cols.start == 0:
+                y16[e] = work.tile([P, S, 4], BF16, name="y16", align_bytes=64)
+            nc.vector.tensor_copy(out=y16[e][:, cols, :], in_=y32[e][:, :, cols].rearrange("p t s -> p s t"))
+
+        def quantise_y(e, cols):
+            span = slice(S * e + cols.start, S * e + cols.stop)
+            nc.vector.quantize_mx(
+                out=y_codes[:, span].bitcast(FP8X4),
+                scales=y_scales[:, span],
+                in_=y16[e][:, cols, :].rearrange("p s t -> p (s t)"),
+            )
+
+        def store_y(e, ts):
+            rows = out_0[e].rearrange("(p t) s -> p t s", t=4)
+            nc.sync.dma_start(out=rows[:, ts, :], in_=y32[e][:, ts, :])
+
+        def store_words(span):
+            nc.sync.dma_start(out=words_out[:, span], in_=y_codes[:, span].bitcast(I32))
+
+        def store_scales(span, engine):
+            for q in range(4):
+                engine.dma_start(
+                    out=out_2[0, 4 * q : 4 * q + 4, span].bitcast(I32),
+                    in_=y_scales[32 * q : 32 * q + 4, span].bitcast(I32),
+                )
+
+        whole = slice(0, S)
+        for s in range(RAW_BUFS):
+            load(s)
+            if s == 1:
+                nc.sync.dma_start(out=gain_sb[:], in_=gain.rearrange("e (p t) -> p e t", t=4))
+                nc.sync.dma_start(out=alpha_sb[:], in_=alpha.partition_broadcast(P))
+        make_identity(nc, ident[:])
+        nc.scalar.activation(out=warm[:], in_=ident[:, 0:1], func=COPY)
+        save_second(0, 0)
+        gather_first(0, 0)
+        save_second(0, 1)
+        gather_first(0, 1)
+
+        last = len(steps) - 1
+        quantised = [0]
+
+        def quantise_until(n):
+            while quantised[0] < n:
+                quantise(*divmod(quantised[0], 4))
+                quantised[0] += 1
+
+        pending, todo, late = [], [], None
+        for s in range(len(steps)):
+            for b in range(4):
+                transposes(s, b)
+            if s + RAW_BUFS <= last:
+                load(s + RAW_BUFS)
+            for b in range(4):
+                if b == ACC_POS:
+                    for m in pending:
+                        scale_out(m, group_items(m))
+                if (s, b) not in V_BANKS:
+                    empty_bank(s, b)
+            finished = [m // 4 for m in pending if m % 4 == 3]
+            pending = [m for m in range(14) if MM_AFTER[m] == s]
+            for e in finished:
+                todo = [(e, 0), (e, 1), (e, 2)]
+            order = VORD_H if s < HEAD else VORD
+            lag = QLAG_H if s < HEAD else QLAG
+            for item in order.split():
+                if item[0] == "s":
+                    save_second(s + 1, int(item[1]))
+                elif item[0] == "g":
+                    gather_first(s + 1, int(item[1]))
+                elif item[0] == "e":
+                    for b in range(4):
+                        if (s, b) in V_BANKS:
+                            empty_bank(s, b)
+                elif item[0] == "q":
+                    quantise_until(4 * s + "abcd".index(item[1]) - lag + 1)
+                else:
+                    if s == FACTOR_STEP:
+                        nc.vector.scalar_tensor_tensor(
+                            out=factor[:],
+                            in0=gain_sb[:],
+                            scalar=1.0 / R,
+                            in1=alpha_sb[:].unsqueeze(2).to_broadcast([P, E, 4]),
+                            op0=MULT,
+                            op1=MULT,
+                        )
+                    for n in range(2 if s == last else 1):
+                        if todo and todo[0][1] < 2:
+                            e, half = todo[0]
+                            round_y(e, slice(256 * half, 256 * (half + 1)))
+                            todo = todo[1:]
+                        elif todo and s != last:
+                            late = todo[0][0]
+                            todo = []
+            if s == last and todo:
+                late = todo[0][0]
+            if late is not None:
+                quantise_y(late, whole)
+            for m in pending:
+                need = [4 * (m // 4) * 4 + 8, 4 * (m // 4) * 4 + 12, 4 * (m // 4) * 4 + 14, 4 * (m // 4) * 4 + 16][m % 4]
+                quantise_until(need)
+                multiply(m, group_items(m))
+            for e in finished:
+                store_y(e, slice(0, 4))
+            if late is not None:
+                store_words(slice(S * late, S * (late + 1)))
+                if late == E - 2:
+                    store_scales(slice(0, S * (E - 1)), nc.sync)
+                late = None
+
+        quantise_until(4 * len(steps))
+        m = 13
+        e = E - 1
+        scale_out(m, group_items(m))
+        store_y(e, slice(0, 2))
+        parts = [slice(0, 256), slice(256, 384), slice(384, 512)] if TAILQ else [slice(0, 256), slice(256, 512)]
+        for n, cols in enumerate(parts):
+            for t in (2, 3):
+                multiply((n, t), [(e, t, cols)], "bank")
+        for n, cols in enumerate(parts):
+            for t in (2, 3):
+                scale_out((n, t), [(e, t, cols)])
+        round_y(e, parts[0])
+        round_y(e, parts[1])
+        quantise_y(e, parts[0])
+        if TAILQ:
+            round_y(e, parts[2])
+        quantise_y(e, parts[1])
+        if TAILQ:
+            quantise_y(e, parts[2])
+        store_y(e, slice(2, 4))
+        store_words(slice(S * e, S * E))
+        store_scales(slice(S * e, S * E), nc.scalar)

@@ -24,20 +24,20 @@ A_FIRST = 1
 BY_TILE = (1, 2)
 FACTOR_STEP = 1
 HEAD = 3
-VORD_H = "qa s0 g0 qb qc s1 g1 e o qd"
-VORD = "s0 qa g0 s1 o g1 qb qc e qd"
-QLAG_H = 1
+VORD_H = "s0 qa g0 qb s1 e o qc g1 qd"
+VORD_X = "s0 qa s1 qb g0 e g1 o qc qd"
+VORD_A = "qa s0 s1 qb qc g0 o g1 qd e"
+VORD_L = "s0 s1 o qa qb e qc qd g0 g1"
+QLAG_H = 2
 MM_AFTER = [m + 2 for m in range(14)]
 SPLIT_Q = (15,)
 QY = 1
 TAILQ = 1
-V_BANKS = ((3, 3), (7, 3), (11, 3), (15, 3))
+V_BANKS = ((3, 3), (7, 3), (11, 3), (15, 1))
 AHEAD_FROM = 99
-QLAG = 1
-VORD_X = "s0 qa g0 s1 qb g1 e o qc qd"
-VORD_A = "s0 qa g0 s1 qb g1 e o qc qd"
+QLAG = 2
 ACC_POS = 0
-SINGLE = 3
+SINGLE = 6
 
 
 def tile_lora_down_scaled_rank_planes_g2_kernel(tc, x, a_down, gain, alpha, out_0, out_1, out_2):
@@ -54,9 +54,10 @@ def tile_lora_down_scaled_rank_planes_g2_kernel(tc, x, a_down, gain, alpha, out_
         ctx.enter_context(tc.manual_schedule())
 
         ident = keep.tile([P, P], F32, name="ident")
-        gain_sb = keep.tile([P, E, 4], BF16, name="gain_sb")
-        alpha_sb = keep.tile([P, E], BF16, name="alpha_sb")
-        factor = keep.tile([P, E, 4], F32, name="factor")
+        gain_sb = keep.tile([E, R], BF16, name="gain_sb")
+        alpha_sb = keep.tile([E, 1], BF16, name="alpha_sb")
+        factor_rows = keep.tile([P, R], F32, name="factor_rows")
+        factor = keep.tile([P, 4, E], F32, name="factor")
         warm = keep.tile([P, 1], F32, name="warm")
         y_codes = keep.tile([P, E * S], U32, name="y_codes", align_bytes=64)
         y_scales = keep.tile([P, E * S], U8, name="y_scales", align_bytes=64)
@@ -187,7 +188,7 @@ def tile_lora_down_scaled_rank_planes_g2_kernel(tc, x, a_down, gain, alpha, out_
                 if e not in y32:
                     y32[e] = work.tile([P, 4, S], F32, name="y32", bufs=E)
                 nc.scalar.activation(
-                    out=y32[e][:, t, cols], in_=acc[key][:, at : at + width], func=COPY, scale=factor[:, e, t : t + 1]
+                    out=y32[e][:, t, cols], in_=acc[key][:, at : at + width], func=COPY, scale=factor[:, t, e : e + 1]
                 )
                 at += width
 
@@ -204,9 +205,9 @@ def tile_lora_down_scaled_rank_planes_g2_kernel(tc, x, a_down, gain, alpha, out_
                 in_=y16[e][:, cols, :].rearrange("p s t -> p (s t)"),
             )
 
-        def store_y(e, ts):
+        def store_y(e, ts, cols=slice(0, S)):
             rows = out_0[e].rearrange("(p t) s -> p t s", t=4)
-            nc.sync.dma_start(out=rows[:, ts, :], in_=y32[e][:, ts, :])
+            nc.sync.dma_start(out=rows[:, ts, cols], in_=y32[e][:, ts, cols])
 
         def store_words(span):
             nc.sync.dma_start(out=words_out[:, span], in_=y_codes[:, span].bitcast(I32))
@@ -221,11 +222,20 @@ def tile_lora_down_scaled_rank_planes_g2_kernel(tc, x, a_down, gain, alpha, out_
         whole = slice(0, S)
         for s in range(RAW_BUFS):
             load(s)
-            if s == 1:
-                nc.sync.dma_start(out=gain_sb[:], in_=gain.rearrange("e (p t) -> p e t", t=4))
-                nc.sync.dma_start(out=alpha_sb[:], in_=alpha.partition_broadcast(P))
+        nc.scalar.dma_start(out=gain_sb[:], in_=gain)
+        with nc.allow_non_contiguous_dma(reason="one alpha to a partition"):
+            nc.scalar.dma_start(out=alpha_sb[:], in_=alpha.rearrange("(e o) -> e o", o=1))
         make_identity(nc, ident[:])
-        nc.scalar.activation(out=warm[:], in_=ident[:, 0:1], func=COPY)
+        nc.vector.memset(warm[:], 0.0)
+        nc.vector.memset(factor_rows[:], 0.0)
+        nc.scalar.activation(out=warm[:], in_=warm[:], func=COPY)
+        nc.vector.tensor_scalar(
+            out=factor_rows[0:E, :], in0=gain_sb[:], scalar1=alpha_sb[:], scalar2=1.0 / R, op0=MULT, op1=MULT
+        )
+        factor_bank = psum.tile([P, 4, P], F32, name="bank", bufs=T_BANKS)
+        for t in range(4):
+            nc.tensor.transpose(factor_bank[:, t, :], factor_rows[:, t::4], ident[:])
+        nc.scalar.copy(out=factor[:], in_=factor_bank[:, :, 0:E])
         save_second(0, 0)
         gather_first(0, 0)
         save_second(0, 1)
@@ -255,7 +265,7 @@ def tile_lora_down_scaled_rank_planes_g2_kernel(tc, x, a_down, gain, alpha, out_
             pending = [m for m in range(14) if MM_AFTER[m] == s]
             for e in finished:
                 todo = [(e, 0), (e, 1), (e, 2)]
-            order = VORD_H if s < HEAD else VORD
+            order = VORD_H if s < HEAD else (VORD_L if s == last else (VORD_X if steps[s][0] == "x" else VORD_A))
             lag = QLAG_H if s < HEAD else QLAG
             for item in order.split():
                 if item[0] == "s":
@@ -269,15 +279,6 @@ def tile_lora_down_scaled_rank_planes_g2_kernel(tc, x, a_down, gain, alpha, out_
                 elif item[0] == "q":
                     quantise_until(4 * s + "abcd".index(item[1]) - lag + 1)
                 else:
-                    if s == FACTOR_STEP:
-                        nc.vector.scalar_tensor_tensor(
-                            out=factor[:],
-                            in0=gain_sb[:],
-                            scalar=1.0 / R,
-                            in1=alpha_sb[:].unsqueeze(2).to_broadcast([P, E, 4]),
-                            op0=MULT,
-                            op1=MULT,
-                        )
                     for n in range(2 if s == last else 1):
                         if todo and todo[0][1] < 2:
                             e, half = todo[0]
@@ -314,14 +315,17 @@ def tile_lora_down_scaled_rank_planes_g2_kernel(tc, x, a_down, gain, alpha, out_
         for n, cols in enumerate(parts):
             for t in (2, 3):
                 scale_out((n, t), [(e, t, cols)])
+            if n == 0:
+                store_y(e, slice(2, 4), cols)
+        store_y(e, slice(2, 4), slice(256, 512))
         round_y(e, parts[0])
         round_y(e, parts[1])
         quantise_y(e, parts[0])
+        store_words(slice(S * e, S * e + 256))
         if TAILQ:
             round_y(e, parts[2])
         quantise_y(e, parts[1])
         if TAILQ:
             quantise_y(e, parts[2])
-        store_y(e, slice(2, 4))
-        store_words(slice(S * e, S * E))
+        store_words(slice(S * e + 256, S * E))
         store_scales(slice(S * e, S * E), nc.scalar)

@@ -23,17 +23,27 @@ FIRST_MM_STEP = 2
 A_FIRST = 1
 BY_TILE = (1, 2)
 FACTOR_STEP = 1
-HEAD = 3
-VORD_H = "s0 qa g0 qb s1 e o qc g1 qd"
-VORD_X = "s0 qa s1 qb g0 e g1 o qc qd"
-VORD_A = "qa s0 s1 qb qc g0 o g1 qd e"
-VORD_L = "s0 s1 o qa qb e qc qd g0 g1"
+HEAD = 5
+STRIDED = 4
+JOINT_FROM = 3
+HALF_LOADS = 2
+WHOLE_ROUND = 0
+ACC_POS2 = 0
+WARM = 0
+KEEP = ()
+FACTOR_AT = 0
+TAIL = 0
+S_ROUND = ()
+VORD_H = "qa qb qc s0 s1 g1 e g0 qd o"
+VORD_X = "qa s0 qb qc s1 g0 o e qd g1"
+VORD_A = "s1 qa s0 qb g0 e qc qd g1 o"
+VORD_L = "e s1 s0 qa o qb qc qd g1 g0"
 QLAG_H = 2
 MM_AFTER = [m + 2 for m in range(14)]
 SPLIT_Q = (15,)
 QY = 1
 TAILQ = 1
-V_BANKS = ((3, 3), (7, 3), (11, 3), (15, 1))
+V_BANKS = ((0, 3), (2, 3), (4, 1), (5, 3), (8, 3), (11, 3))
 AHEAD_FROM = 99
 QLAG = 2
 ACC_POS = 0
@@ -74,26 +84,33 @@ def tile_lora_down_scaled_rank_planes_g2_kernel(tc, x, a_down, gain, alpha, out_
                 src = a_down[e].rearrange("(p t) k -> p t k", t=4)[:, 2 * h : 2 * h + 2, :]
             if s < SINGLE:
                 for j in range(2):
-                    nc.sync.dma_start(out=raw[s][:, j, :], in_=src[:, j, :])
+                    if 2 * s + j < HALF_LOADS:
+                        for c in range(2):
+                            ks = slice(c * D // 2, (c + 1) * D // 2)
+                            nc.sync.dma_start(out=raw[s][:, j, ks], in_=src[:, j, ks])
+                    else:
+                        nc.sync.dma_start(out=raw[s][:, j, :], in_=src[:, j, :])
             else:
                 nc.sync.dma_start(out=raw[s][:], in_=src)
 
-        def halves(s, j):
-            return raw[s][:, j, :].rearrange("p (h b u i) -> p h b u i", h=2, u=2, i=16)
-
         def save_second(s, j):
-            if s >= len(steps):
+            if s >= len(steps) or s < STRIDED or (s >= JOINT_FROM and j == 1):
                 return
-            second[s, j] = work.tile([P, D // 2], BF16, name="second", bufs=6, align_bytes=64)
+            if j == 0:
+                second[s] = work.tile([P, 2, D // 2], BF16, name="second", bufs=3, align_bytes=64)
+            js = slice(0, 2) if s >= JOINT_FROM else slice(j, j + 1)
+            blocks = raw[s][:, js, :].rearrange("p j (h b u i) -> p j h b u i", h=2, u=2, i=16)
             nc.vector.tensor_copy(
-                out=second[s, j][:].rearrange("p (b h i) -> p h b i", h=2, i=16),
-                in_=halves(s, j)[:, :, :, 1, :],
+                out=second[s][:, js, :].rearrange("p j (b h i) -> p j h b i", h=2, i=16),
+                in_=blocks[:, :, :, :, 1, :],
             )
 
         def gather_first(s, j):
-            if s >= len(steps):
+            if s >= len(steps) or s < STRIDED or (s >= JOINT_FROM and j == 1):
                 return
-            nc.vector.tensor_copy(out=halves(s, j)[:, 0, :, 1, :], in_=halves(s, j)[:, 1, :, 0, :])
+            js = slice(0, 2) if s >= JOINT_FROM else slice(j, j + 1)
+            blocks = raw[s][:, js, :].rearrange("p j (h b u i) -> p j h b u i", h=2, u=2, i=16)
+            nc.vector.tensor_copy(out=blocks[:, :, 0, :, 1, :], in_=blocks[:, :, 1, :, 0, :])
 
         def bank_items(s, b):
             if steps[s][0] == "x" and s not in BY_TILE:
@@ -103,10 +120,15 @@ def tile_lora_down_scaled_rank_planes_g2_kernel(tc, x, a_down, gain, alpha, out_
         def transposes(s, b):
             banks[s, b] = psum.tile([P, 2, 2, P], F32, name="bank", bufs=T_BANKS)
             for n, (j, g) in enumerate(bank_items(s, b)):
-                first_words = raw[s][:, j, : D // 2].bitcast(F32)
-                second_words = second[s, j][:].bitcast(F32)
-                for u, words in enumerate((first_words, second_words)):
-                    nc.tensor.transpose(banks[s, b][:, n, u, :], words[:, P * g : P * (g + 1)], ident[:])
+                if s < STRIDED:
+                    words = raw[s][:, j, :].bitcast(F32)
+                    windows = [words[:, 2 * P * g + u : 2 * P * (g + 1) : 2] for u in range(2)]
+                else:
+                    first_words = raw[s][:, j, : D // 2].bitcast(F32)
+                    second_words = second[s][:, j, :].bitcast(F32)
+                    windows = [words[:, P * g : P * (g + 1)] for words in (first_words, second_words)]
+                for u in range(2):
+                    nc.tensor.transpose(banks[s, b][:, n, u, :], windows[u], ident[:])
 
         def empty_bank(s, b):
             if b % 2 == 0:
@@ -122,23 +144,23 @@ def tile_lora_down_scaled_rank_planes_g2_kernel(tc, x, a_down, gain, alpha, out_
             kind, e, h = steps[s]
             if kind == "x":
                 if h == 0 and b == 0:
-                    x_codes[e] = work.tile([P, PASSES, S], U32, name="x_codes", align_bytes=64)
-                    x_scales[e] = work.tile([P, PASSES, S], U8, name="x_scales", align_bytes=64)
+                    x_codes[e] = work.tile([P, 2, PASSES, 256], U32, name="x_codes", align_bytes=64)
+                    x_scales[e] = work.tile([P, 2, PASSES, 256], U8, name="x_scales", align_bytes=64)
                 if s in BY_TILE:
                     for n, (j, g) in enumerate(bank_items(s, b)):
-                        cols = slice(256 * h + P * j, 256 * h + P * (j + 1))
+                        cols = slice(P * j, P * (j + 1))
                         nc.vector.quantize_mx(
-                            out=x_codes[e][:, g, cols].bitcast(FP8X4),
-                            scales=x_scales[e][:, g, cols],
+                            out=x_codes[e][:, h, g, cols].bitcast(FP8X4),
+                            scales=x_scales[e][:, h, g, cols],
                             in_=grouped[s, b // 2][:, b % 2, 4 * P * n : 4 * P * (n + 1)],
                         )
                     return
-                cols = slice(256 * h, 256 * (h + 1))
-                nc.vector.quantize_mx(
-                    out=x_codes[e][:, b, cols].bitcast(FP8X4),
-                    scales=x_scales[e][:, b, cols],
-                    in_=grouped[s, b // 2][:, b % 2, :],
-                )
+                if b % 2 == 1:
+                    nc.vector.quantize_mx(
+                        out=x_codes[e][:, h, b - 1 : b + 1, :].rearrange("p g c -> p (g c)").bitcast(FP8X4),
+                        scales=x_scales[e][:, h, b - 1 : b + 1, :].rearrange("p g c -> p (g c)"),
+                        in_=grouped[s, b // 2][:].rearrange("p n c -> p (n c)"),
+                    )
                 return
             t = 2 * h + b // 2
             if b % 2 == (0 if s in SPLIT_Q else 1):
@@ -162,39 +184,39 @@ def tile_lora_down_scaled_rank_planes_g2_kernel(tc, x, a_down, gain, alpha, out_
             e, n = divmod(m, 4)
             if n < 2:
                 return [(e, t, slice(256 * n, 256 * (n + 1))) for t in range(2)]
-            return [(e, n, slice(0, S))]
+            return [(e, n, slice(0, 256)), (e, n, slice(256, 512))]
 
-        def multiply(key, items, tag="acc"):
-            acc[key] = psum.tile([P, S], F32, name=tag, bufs=8 - T_BANKS if tag == "acc" else T_BANKS)
-            at = 0
-            for e, t, cols in items:
-                width = cols.stop - cols.start
-                for g in range(PASSES):
-                    nc.tensor.matmul_mx(
-                        out=acc[key][:, at : at + width],
-                        lhsT=a_codes[e, t][:, P * g : P * (g + 1)].bitcast(FP8X4),
-                        lhsT_scale=a_scales[e, t][:, P * g : P * (g + 1)],
-                        rhs=x_codes[e][:, g, cols].bitcast(FP8X4),
-                        rhs_scale=x_scales[e][:, g, cols],
-                        start=(g == 0),
-                        stop=(g == PASSES - 1),
-                    )
-                at += width
+        def finished_rows(m):
+            e, n = divmod(m, 4)
+            return [[], [(e, 0), (e, 1)], [(e, 2)], [(e, 3)]][n]
 
-        def scale_out(key, items):
-            at = 0
-            for e, t, cols in items:
-                width = cols.stop - cols.start
-                if e not in y32:
-                    y32[e] = work.tile([P, 4, S], F32, name="y32", bufs=E)
-                nc.scalar.activation(
-                    out=y32[e][:, t, cols], in_=acc[key][:, at : at + width], func=COPY, scale=factor[:, t, e : e + 1]
+        def multiply(e, t, cols, key, tag, passes=range(PASSES)):
+            if key not in acc:
+                acc[key] = psum.tile([P, S], F32, name=tag, bufs=8 - T_BANKS if tag == "acc" else T_BANKS)
+            h = cols.start // 256
+            window = slice(cols.start - 256 * h, cols.stop - 256 * h)
+            for g in passes:
+                nc.tensor.matmul_mx(
+                    out=acc[key][:, cols],
+                    lhsT=a_codes[e, t][:, P * g : P * (g + 1)].bitcast(FP8X4),
+                    lhsT_scale=a_scales[e, t][:, P * g : P * (g + 1)],
+                    rhs=x_codes[e][:, h, g, window].bitcast(FP8X4),
+                    rhs_scale=x_scales[e][:, h, g, window],
+                    start=(g == 0),
+                    stop=(g == PASSES - 1),
                 )
-                at += width
+
+        def scale_out(e, t, cols, key):
+            if e not in y32:
+                y32[e] = work.tile([P, 4, S], F32, name="y32", bufs=E)
+            nc.scalar.activation(out=y32[e][:, t, cols], in_=acc[key][:, cols], func=COPY, scale=factor[:, t, e : e + 1])
 
         def round_y(e, cols):
             if cols.start == 0:
                 y16[e] = work.tile([P, S, 4], BF16, name="y16", align_bytes=64)
+            if e == E - 1 and cols.start in S_ROUND:
+                nc.scalar.copy(out=y16[e][:, cols, :], in_=y32[e][:, :, cols].rearrange("p t s -> p s t"))
+                return
             nc.vector.tensor_copy(out=y16[e][:, cols, :], in_=y32[e][:, :, cols].rearrange("p t s -> p s t"))
 
         def quantise_y(e, cols):
@@ -227,15 +249,42 @@ def tile_lora_down_scaled_rank_planes_g2_kernel(tc, x, a_down, gain, alpha, out_
             nc.scalar.dma_start(out=alpha_sb[:], in_=alpha.rearrange("(e o) -> e o", o=1))
         make_identity(nc, ident[:])
         nc.vector.memset(warm[:], 0.0)
+        if WARM:
+            zeros = keep.tile([P, 4 * S], BF16, name="zeros", align_bytes=64)
+            zero_codes = keep.tile([P, S], U32, name="zero_codes", align_bytes=64)
+            zero_scales = keep.tile([P, S], U8, name="zero_scales", align_bytes=64)
+            spare = psum.tile([P, S], F32, name="acc", bufs=8 - T_BANKS)
+            nc.vector.memset(zeros[:].bitcast(I32), 0)
         nc.vector.memset(factor_rows[:], 0.0)
+        if WARM:
+            nc.vector.quantize_mx(out=zero_codes[:].bitcast(FP8X4), scales=zero_scales[:], in_=zeros[:])
+
+        def idle_pass():
+            nc.tensor.matmul_mx(
+                out=spare[:],
+                lhsT=zero_codes[:, :P].bitcast(FP8X4),
+                lhsT_scale=zero_scales[:, :P],
+                rhs=zero_codes[:].bitcast(FP8X4),
+                rhs_scale=zero_scales[:],
+                start=True,
+                stop=True,
+            )
+
+        for n in range(WARM):
+            idle_pass()
         nc.scalar.activation(out=warm[:], in_=warm[:], func=COPY)
         nc.vector.tensor_scalar(
             out=factor_rows[0:E, :], in0=gain_sb[:], scalar1=alpha_sb[:], scalar2=1.0 / R, op0=MULT, op1=MULT
         )
-        factor_bank = psum.tile([P, 4, P], F32, name="bank", bufs=T_BANKS)
-        for t in range(4):
-            nc.tensor.transpose(factor_bank[:, t, :], factor_rows[:, t::4], ident[:])
-        nc.scalar.copy(out=factor[:], in_=factor_bank[:, :, 0:E])
+
+        def turn_factor():
+            factor_bank = psum.tile([P, 4, P], F32, name="bank", bufs=T_BANKS)
+            for t in range(4):
+                nc.tensor.transpose(factor_bank[:, t, :], factor_rows[:, t::4], ident[:])
+            nc.scalar.copy(out=factor[:], in_=factor_bank[:, :, 0:E])
+
+        if FACTOR_AT < 0:
+            turn_factor()
         save_second(0, 0)
         gather_first(0, 0)
         save_second(0, 1)
@@ -253,18 +302,23 @@ def tile_lora_down_scaled_rank_planes_g2_kernel(tc, x, a_down, gain, alpha, out_
         for s in range(len(steps)):
             for b in range(4):
                 transposes(s, b)
+                if WARM and (s, b) in KEEP:
+                    idle_pass()
             if s + RAW_BUFS <= last:
                 load(s + RAW_BUFS)
             for b in range(4):
-                if b == ACC_POS:
-                    for m in pending:
-                        scale_out(m, group_items(m))
+                for m in pending:
+                    for n, (e, t) in enumerate(finished_rows(m)):
+                        if b == (ACC_POS, ACC_POS2)[n]:
+                            scale_out(e, t, whole, (e, t))
                 if (s, b) not in V_BANKS:
                     empty_bank(s, b)
+            if s == FACTOR_AT:
+                turn_factor()
             finished = [m // 4 for m in pending if m % 4 == 3]
             pending = [m for m in range(14) if MM_AFTER[m] == s]
             for e in finished:
-                todo = [(e, 0), (e, 1), (e, 2)]
+                todo = [(e, 1), (e, 2)] if WHOLE_ROUND else [(e, 0), (e, 1), (e, 2)]
             order = VORD_H if s < HEAD else (VORD_L if s == last else (VORD_X if steps[s][0] == "x" else VORD_A))
             lag = QLAG_H if s < HEAD else QLAG
             for item in order.split():
@@ -282,7 +336,7 @@ def tile_lora_down_scaled_rank_planes_g2_kernel(tc, x, a_down, gain, alpha, out_
                     for n in range(2 if s == last else 1):
                         if todo and todo[0][1] < 2:
                             e, half = todo[0]
-                            round_y(e, slice(256 * half, 256 * (half + 1)))
+                            round_y(e, whole if WHOLE_ROUND else slice(256 * half, 256 * (half + 1)))
                             todo = todo[1:]
                         elif todo and s != last:
                             late = todo[0][0]
@@ -294,7 +348,8 @@ def tile_lora_down_scaled_rank_planes_g2_kernel(tc, x, a_down, gain, alpha, out_
             for m in pending:
                 need = [4 * (m // 4) * 4 + 8, 4 * (m // 4) * 4 + 12, 4 * (m // 4) * 4 + 14, 4 * (m // 4) * 4 + 16][m % 4]
                 quantise_until(need)
-                multiply(m, group_items(m))
+                for e, t, cols in group_items(m):
+                    multiply(e, t, cols, (e, t), "acc")
             for e in finished:
                 store_y(e, slice(0, 4))
             if late is not None:
@@ -306,18 +361,31 @@ def tile_lora_down_scaled_rank_planes_g2_kernel(tc, x, a_down, gain, alpha, out_
         quantise_until(4 * len(steps))
         m = 13
         e = E - 1
-        scale_out(m, group_items(m))
+        for t in range(2):
+            scale_out(e, t, whole, (e, t))
         store_y(e, slice(0, 2))
         parts = [slice(0, 256), slice(256, 384), slice(384, 512)] if TAILQ else [slice(0, 256), slice(256, 512)]
-        for n, cols in enumerate(parts):
-            for t in (2, 3):
-                multiply((n, t), [(e, t, cols)], "bank")
-        for n, cols in enumerate(parts):
-            for t in (2, 3):
-                scale_out((n, t), [(e, t, cols)])
-            if n == 0:
-                store_y(e, slice(2, 4), cols)
-        store_y(e, slice(2, 4), slice(256, 512))
+        if TAIL == 0:
+            for n, cols in enumerate(parts):
+                for t in (2, 3):
+                    multiply(e, t, cols, (e, t, n), "bank")
+            for n, cols in enumerate(parts):
+                for t in (2, 3):
+                    scale_out(e, t, cols, (e, t, n))
+                if n == 0:
+                    store_y(e, slice(2, 4), cols)
+            store_y(e, slice(2, 4), slice(256, 512))
+        else:
+            for h in range(2):
+                multiply(e, 2, slice(256 * h, 256 * (h + 1)), (e, 2), "bank")
+            for passes in (range(2), range(2, 4)):
+                for n, cols in enumerate(parts):
+                    multiply(e, 3, cols, (e, 3, n), "bank", passes)
+            scale_out(e, 2, whole, (e, 2))
+            store_y(e, slice(2, 3))
+            for n, cols in enumerate(parts):
+                scale_out(e, 3, cols, (e, 3, n))
+            store_y(e, slice(3, 4))
         round_y(e, parts[0])
         round_y(e, parts[1])
         quantise_y(e, parts[0])

@@ -23,31 +23,32 @@ FIRST_MM_STEP = 2
 A_FIRST = 1
 BY_TILE = (1, 2)
 FACTOR_STEP = 1
-HEAD = 5
-STRIDED = 4
-JOINT_FROM = 3
-HALF_LOADS = 2
+HEAD = 2
+STRIDED = 0
+JOINT_FROM = 4
+HALF_LOADS = 0
 WHOLE_ROUND = 0
 ACC_POS2 = 0
-WARM = 0
-KEEP = ()
+WARM = 4
+KEEP = ((0, 3), (0, 3), (1, 3), (1, 3))
 FACTOR_AT = 0
 TAIL = 0
+PAIR = 1
 S_ROUND = ()
-VORD_H = "qa qb qc s0 s1 g1 e g0 qd o"
-VORD_X = "qa s0 qb qc s1 g0 o e qd g1"
-VORD_A = "s1 qa s0 qb g0 e qc qd g1 o"
-VORD_L = "e s1 s0 qa o qb qc qd g1 g0"
-QLAG_H = 2
+VORD_H = "s0 g0 qa o s1 e qb g1 qc qd"
+VORD_X = "s0 qa qb g0 o s1 qc g1 e qd"
+VORD_A = "qa s1 s0 qb g0 g1 qc o qd e"
+VORD_L = "s0 e qa o g0 qb s1 g1 qc qd"
+QLAG_H = 1
 MM_AFTER = [m + 2 for m in range(14)]
 SPLIT_Q = (15,)
 QY = 1
 TAILQ = 1
-V_BANKS = ((0, 3), (2, 3), (4, 1), (5, 3), (8, 3), (11, 3))
+V_BANKS = ((3, 3), (4, 3), (7, 3), (11, 3))
 AHEAD_FROM = 99
 QLAG = 2
 ACC_POS = 0
-SINGLE = 6
+SINGLE = 4
 
 
 def tile_lora_down_scaled_rank_planes_g2_kernel(tc, x, a_down, gain, alpha, out_0, out_1, out_2):
@@ -118,7 +119,11 @@ def tile_lora_down_scaled_rank_planes_g2_kernel(tc, x, a_down, gain, alpha, out_
             return [(b // 2, 2 * (b % 2)), (b // 2, 2 * (b % 2) + 1)]
 
         def transposes(s, b):
-            banks[s, b] = psum.tile([P, 2, 2, P], F32, name="bank", bufs=T_BANKS)
+            if not PAIR:
+                banks[s, b] = psum.tile([P, 2, 2, P], F32, name="bank", bufs=T_BANKS)
+            elif b % 2 == 0:
+                pair = psum.tile([P, 2, 2, 2, P], F32, name="bank", bufs=T_BANKS // 2)
+                banks[s, b], banks[s, b + 1] = pair[:, 0], pair[:, 1]
             for n, (j, g) in enumerate(bank_items(s, b)):
                 if s < STRIDED:
                     words = raw[s][:, j, :].bitcast(F32)
@@ -134,7 +139,7 @@ def tile_lora_down_scaled_rank_planes_g2_kernel(tc, x, a_down, gain, alpha, out_
             if b % 2 == 0:
                 grouped[s, b // 2] = work.tile([P, 2, 4 * 2 * P], BF16, name="grouped", bufs=4, align_bytes=64)
             dst = grouped[s, b // 2][:, b % 2, :].bitcast(F32).rearrange("p (n r u) -> p n r u", n=2, u=2)
-            src = banks[s, b][:].rearrange("p n u r -> p n r u")
+            src = banks[s, b].rearrange("p n u r -> p n r u")
             if (s, b) in V_BANKS:
                 nc.vector.tensor_copy(out=dst, in_=src)
             else:
@@ -278,7 +283,7 @@ def tile_lora_down_scaled_rank_planes_g2_kernel(tc, x, a_down, gain, alpha, out_
         )
 
         def turn_factor():
-            factor_bank = psum.tile([P, 4, P], F32, name="bank", bufs=T_BANKS)
+            factor_bank = psum.tile([P, 4, P], F32, name="acc", bufs=8 - T_BANKS)
             for t in range(4):
                 nc.tensor.transpose(factor_bank[:, t, :], factor_rows[:, t::4], ident[:])
             nc.scalar.copy(out=factor[:], in_=factor_bank[:, :, 0:E])
@@ -302,8 +307,9 @@ def tile_lora_down_scaled_rank_planes_g2_kernel(tc, x, a_down, gain, alpha, out_
         for s in range(len(steps)):
             for b in range(4):
                 transposes(s, b)
-                if WARM and (s, b) in KEEP:
-                    idle_pass()
+                for at in KEEP:
+                    if WARM and at == (s, b):
+                        idle_pass()
             if s + RAW_BUFS <= last:
                 load(s + RAW_BUFS)
             for b in range(4):
@@ -367,6 +373,9 @@ def tile_lora_down_scaled_rank_planes_g2_kernel(tc, x, a_down, gain, alpha, out_
         parts = [slice(0, 256), slice(256, 384), slice(384, 512)] if TAILQ else [slice(0, 256), slice(256, 512)]
         if TAIL == 0:
             for n, cols in enumerate(parts):
+                if PAIR:
+                    pair = psum.tile([P, 2, S], F32, name="bank", bufs=T_BANKS // 2)
+                    acc[e, 2, n], acc[e, 3, n] = pair[:, 0, :], pair[:, 1, :]
                 for t in (2, 3):
                     multiply(e, t, cols, (e, t, n), "bank")
             for n, cols in enumerate(parts):

@@ -17,211 +17,188 @@ COPY = mybir.ActivationFunctionType.Copy
 
 P = 128
 PASSES = 4
-RAW_BUFS = 12
-T_BANKS = 6
-FIRST_MM_STEP = 2
-A_FIRST = 1
-BY_TILE = (1, 2)
-FACTOR_STEP = 1
-HEAD = 2
-STRIDED = 0
-JOINT_FROM = 4
-HALF_LOADS = 0
-WHOLE_ROUND = 0
-ACC_POS2 = 0
-WARM = 4
-KEEP = ((0, 3), (0, 3), (1, 3), (1, 3))
-FACTOR_AT = 0
-TAIL = 0
-PAIR = 1
-S_ROUND = ()
-VORD_H = "s0 g0 qa o s1 e qb g1 qc qd"
-VORD_X = "s0 qa qb g0 o s1 qc g1 e qd"
-VORD_A = "qa s1 s0 qb g0 g1 qc o qd e"
-VORD_L = "s0 e qa o g0 qb s1 g1 qc qd"
-QLAG_H = 1
-MM_AFTER = [m + 2 for m in range(14)]
-SPLIT_Q = (15,)
-QY = 1
-TAILQ = 1
-V_BANKS = ((3, 3), (4, 3), (7, 3), (11, 3))
-AHEAD_FROM = 99
-QLAG = 2
-ACC_POS = 0
-SINGLE = 4
+HALF = 16
+FRONT = 32
+ROW = FRONT + D + 64
+RAW_BUFS = 10
+TAIL_TS = ((0,), (1,), (2,), (3,))
+SINGLE = 8
+ROUND_COLS = 128
+TAIL_V = ()
+FACTOR_AT = 2
+V_BANKS = ((8, 0), (9, 0), (10, 0), (11, 0), (12, 0), (13, 0), (14, 0))
+HOLD = [2] * 8 + [1, 1, 0, 1, 0, 1, 0]
+SORT_AT = [()] * 8 + [(-1,), (-1, 2), (3, 5), (1, 4), (3, 5), (1, 4), ()]
+GROUPED = 10
 
 
 def tile_lora_down_scaled_rank_planes_g2_kernel(tc, x, a_down, gain, alpha, out_0, out_1, out_2):
     nc = tc.nc
-    steps = []
-    for e in range(E):
-        steps += [("a", e, 0), ("x", e, 0), ("x", e, 1), ("a", e, 1)] if e < A_FIRST else [("x", e, 0), ("a", e, 0), ("x", e, 1), ("a", e, 1)]
+    last_e = E - 1
+    first_half, second_half, whole = slice(0, 256), slice(256, 512), slice(0, S)
+    runs = [
+        ([("a", 0, 0, 1)], []),
+        ([("x", 0, 0, 1)], []),
+        ([("x", 0, 1, 1)], []),
+        ([("a", 0, 1, 1)], []),
+        ([("x", 0, 2, 1)], [(0, (0,), first_half)]),
+        ([("x", 0, 3, 1)], [(0, (1,), first_half)]),
+        ([("a", 0, 2, 1)], []),
+        ([("a", 0, 3, 1)], [(0, (0, 1), second_half)]),
+        ([("x", 1, 0, 2)], [(0, (2,), whole)]),
+        ([("x", 1, 2, 2)], [(0, (3,), whole)]),
+        ([("a", 1, 0, 2), ("a", 1, 2, 2)], [(1, (0,), whole), (1, (1,), whole)]),
+        ([("x", 2, 0, 2), ("x", 2, 2, 2)], [(1, (2,), whole), (1, (3,), whole)]),
+        ([("a", 2, 0, 2), ("a", 2, 2, 2)], [(2, (0,), whole), (2, (1,), whole)]),
+        ([("a", 3, 0, 2), ("x", 3, 0, 2)], [(2, (2,), whole), (2, (3,), whole)]),
+        (
+            [("a", 3, 2, 2), ("x", 3, 2, 2)],
+            [(3, (0, 1), first_half), (3, (2, 3), first_half), (3, (0, 1, 2, 3), slice(256, 384))]
+            + [(3, ts, slice(384, 512)) for ts in TAIL_TS],
+        ),
+    ]
+    units = [unit for run, products in runs for unit in run]
+    last = len(units) - 1
+
     words_out = out_1[0].rearrange("p m t -> p (m t)").bitcast(I32)
 
     with ExitStack() as ctx:
         keep = ctx.enter_context(tc.tile_pool(name="keep", bufs=1))
         work = ctx.enter_context(tc.tile_pool(name="work", bufs=2))
-        psum = ctx.enter_context(tc.psum_pool(name="psum", bufs=2))
+        psum = ctx.enter_context(tc.psum_pool(name="psum", bufs=8))
         ctx.enter_context(tc.manual_schedule())
 
         ident = keep.tile([P, P], F32, name="ident")
         gain_sb = keep.tile([E, R], BF16, name="gain_sb")
         alpha_sb = keep.tile([E, 1], BF16, name="alpha_sb")
-        factor_rows = keep.tile([P, R], F32, name="factor_rows")
+        alpha_over_rank = keep.tile([E, 1], F32, name="alpha_over_rank")
+        factor_rows = keep.tile([P, 4, P], F32, name="factor_rows")
         factor = keep.tile([P, 4, E], F32, name="factor")
-        warm = keep.tile([P, 1], F32, name="warm")
         y_codes = keep.tile([P, E * S], U32, name="y_codes", align_bytes=64)
         y_scales = keep.tile([P, E * S], U8, name="y_scales", align_bytes=64)
 
-        raw, second, banks, grouped = {}, {}, {}, {}
-        x_codes, x_scales, a_codes, a_scales, acc, y32, y16 = {}, {}, {}, {}, {}, {}, {}
+        raw, windows, grouped = {}, {}, {}
+        x_codes, x_scales, a_codes, a_scales, y32, y16 = {}, {}, {}, {}, {}, {}
 
         def load(s):
-            kind, e, h = steps[s]
-            raw[s] = work.tile([P, 2, D], BF16, name="raw", bufs=RAW_BUFS, align_bytes=64)
+            kind, e, first, count = units[s]
             if kind == "x":
-                src = x[e, 256 * h : 256 * (h + 1), :].rearrange("(j p) k -> p j k", p=P)
+                src = x[e, P * first : P * (first + count), :].rearrange("(j p) k -> p j k", p=P)
             else:
-                src = a_down[e].rearrange("(p t) k -> p t k", t=4)[:, 2 * h : 2 * h + 2, :]
-            if s < SINGLE:
-                for j in range(2):
-                    if 2 * s + j < HALF_LOADS:
-                        for c in range(2):
-                            ks = slice(c * D // 2, (c + 1) * D // 2)
-                            nc.sync.dma_start(out=raw[s][:, j, ks], in_=src[:, j, ks])
-                    else:
-                        nc.sync.dma_start(out=raw[s][:, j, :], in_=src[:, j, :])
+                src = a_down[e].rearrange("(p t) k -> p t k", t=4)[:, first : first + count, :]
+            if count == 1:
+                raw[s] = work.tile([P, D], BF16, name="lone", bufs=SINGLE, align_bytes=64)
+                nc.sync.dma_start(out=raw[s][:], in_=src[:, 0, :])
             else:
-                nc.sync.dma_start(out=raw[s][:], in_=src)
+                raw[s] = work.tile([P, 2, ROW], BF16, name="raw", bufs=RAW_BUFS, align_bytes=64)
+                nc.sync.dma_start(out=raw[s][:, :, FRONT : FRONT + D], in_=src)
 
-        def save_second(s, j):
-            if s >= len(steps) or s < STRIDED or (s >= JOINT_FROM and j == 1):
-                return
-            if j == 0:
-                second[s] = work.tile([P, 2, D // 2], BF16, name="second", bufs=3, align_bytes=64)
-            js = slice(0, 2) if s >= JOINT_FROM else slice(j, j + 1)
-            blocks = raw[s][:, js, :].rearrange("p j (h b u i) -> p j h b u i", h=2, u=2, i=16)
-            nc.vector.tensor_copy(
-                out=second[s][:, js, :].rearrange("p j (b h i) -> p j h b i", h=2, i=16),
-                in_=blocks[:, :, :, :, 1, :],
-            )
+        def sort_pair(s):
+            halves = raw[s][:, :, FRONT : FRONT + D].rearrange("p j (r b u i) -> p j b r u i", r=2, u=2, i=HALF)
+            span = raw[s][:, :, FRONT - HALF : FRONT - HALF + 2 * (D // 2 + 2 * HALF)]
+            dst = span.rearrange("p j (r c i) -> p j c r i", r=2, i=HALF)[:, :, 0:64:2, :, :]
+            nc.vector.tensor_copy(out=dst, in_=halves[:, :, :, ::-1, 1, :])
+            for j in range(2):
+                windows[s, j] = [
+                    raw[s][:, j, FRONT + D // 2 : FRONT + D].bitcast(F32),
+                    raw[s][:, j, FRONT - HALF : FRONT - HALF + D // 2].bitcast(F32),
+                ]
 
-        def gather_first(s, j):
-            if s >= len(steps) or s < STRIDED or (s >= JOINT_FROM and j == 1):
-                return
-            js = slice(0, 2) if s >= JOINT_FROM else slice(j, j + 1)
-            blocks = raw[s][:, js, :].rearrange("p j (h b u i) -> p j h b u i", h=2, u=2, i=16)
-            nc.vector.tensor_copy(out=blocks[:, :, 0, :, 1, :], in_=blocks[:, :, 1, :, 0, :])
+        def sort_single(s):
+            side = work.tile([P, 2, D // 2], BF16, name="side", bufs=3, align_bytes=64)
+            halves = raw[s][:].rearrange("p (b u i) -> p u b i", u=2, i=HALF)
+            nc.vector.tensor_copy(out=side[:].rearrange("p u (b i) -> p u b i", i=HALF), in_=halves)
+            windows[s, 0] = [side[:, w, :].bitcast(F32) for w in range(2)]
 
-        def bank_items(s, b):
-            if steps[s][0] == "x" and s not in BY_TILE:
-                return [(0, b), (1, b)]
-            return [(b // 2, 2 * (b % 2)), (b // 2, 2 * (b % 2) + 1)]
-
-        def transposes(s, b):
-            if not PAIR:
-                banks[s, b] = psum.tile([P, 2, 2, P], F32, name="bank", bufs=T_BANKS)
-            elif b % 2 == 0:
-                pair = psum.tile([P, 2, 2, 2, P], F32, name="bank", bufs=T_BANKS // 2)
-                banks[s, b], banks[s, b + 1] = pair[:, 0], pair[:, 1]
-            for n, (j, g) in enumerate(bank_items(s, b)):
-                if s < STRIDED:
-                    words = raw[s][:, j, :].bitcast(F32)
-                    windows = [words[:, 2 * P * g + u : 2 * P * (g + 1) : 2] for u in range(2)]
+        def sort(s):
+            if s <= last and (s, 0) not in windows:
+                if units[s][3] == 1:
+                    sort_single(s)
                 else:
-                    first_words = raw[s][:, j, : D // 2].bitcast(F32)
-                    second_words = second[s][:, j, :].bitcast(F32)
-                    windows = [words[:, P * g : P * (g + 1)] for words in (first_words, second_words)]
-                for u in range(2):
-                    nc.tensor.transpose(banks[s, b][:, n, u, :], windows[u], ident[:])
+                    sort_pair(s)
 
-        def empty_bank(s, b):
-            if b % 2 == 0:
-                grouped[s, b // 2] = work.tile([P, 2, 4 * 2 * P], BF16, name="grouped", bufs=4, align_bytes=64)
-            dst = grouped[s, b // 2][:, b % 2, :].bitcast(F32).rearrange("p (n r u) -> p n r u", n=2, u=2)
-            src = banks[s, b].rearrange("p n u r -> p n r u")
-            if (s, b) in V_BANKS:
+        def by_pass(s):
+            return units[s][0] == "x" and units[s][3] == 2 and s != last
+
+        def turn(s, b, on_vector):
+            bank = psum.tile([P, 2, 2, P], F32, name="bank")
+            items = [(0, b), (1, b)] if by_pass(s) else [(b // 2, 2 * (b % 2)), (b // 2, 2 * (b % 2) + 1)]
+            for n, (j, g) in enumerate(items):
+                for u in range(2):
+                    nc.tensor.transpose(bank[:, n, u, :], windows[s, j][u][:, P * g : P * (g + 1)], ident[:])
+            grouped[s, b] = work.tile([P, 4 * 2 * P], BF16, name="grouped", bufs=GROUPED, align_bytes=64)
+            dst = grouped[s, b][:].bitcast(F32).rearrange("p (n r u) -> p n r u", n=2, u=2)
+            src = bank[:].rearrange("p n u r -> p n r u")
+            if on_vector:
                 nc.vector.tensor_copy(out=dst, in_=src)
             else:
                 nc.scalar.copy(out=dst, in_=src)
 
+        def x_span(e, g, cols):
+            if e != last_e:
+                return slice(S * g + cols.start, S * g + cols.stop)
+            if cols.start == 0:
+                return slice(256 * g, 256 * (g + 1))
+            first = 1024 + 4 * (cols.start - 256) + P * g
+            return slice(first, first + P)
+
         def quantise(s, b):
-            kind, e, h = steps[s]
+            kind, e, first, count = units[s]
             if kind == "x":
-                if h == 0 and b == 0:
-                    x_codes[e] = work.tile([P, 2, PASSES, 256], U32, name="x_codes", align_bytes=64)
-                    x_scales[e] = work.tile([P, 2, PASSES, 256], U8, name="x_scales", align_bytes=64)
-                if s in BY_TILE:
-                    for n, (j, g) in enumerate(bank_items(s, b)):
-                        cols = slice(P * j, P * (j + 1))
-                        nc.vector.quantize_mx(
-                            out=x_codes[e][:, h, g, cols].bitcast(FP8X4),
-                            scales=x_scales[e][:, h, g, cols],
-                            in_=grouped[s, b // 2][:, b % 2, 4 * P * n : 4 * P * (n + 1)],
-                        )
-                    return
-                if b % 2 == 1:
-                    nc.vector.quantize_mx(
-                        out=x_codes[e][:, h, b - 1 : b + 1, :].rearrange("p g c -> p (g c)").bitcast(FP8X4),
-                        scales=x_scales[e][:, h, b - 1 : b + 1, :].rearrange("p g c -> p (g c)"),
-                        in_=grouped[s, b // 2][:].rearrange("p n c -> p (n c)"),
+                if first == 0 and b == 0:
+                    x_codes[e] = work.tile([P, PASSES * S], U32, name="x_codes", align_bytes=64)
+                    x_scales[e] = work.tile([P, PASSES * S], U8, name="x_scales", align_bytes=64)
+                codes, scales = x_codes[e], x_scales[e]
+                if count == 1:
+                    spans = [slice(S * g + P * first, S * g + P * (first + 1)) for g in (2 * b, 2 * b + 1)]
+                elif by_pass(s):
+                    spans = [x_span(e, b, slice(P * first, P * (first + 2)))]
+                else:
+                    spans = [slice(1024 + 256 * b, 1280 + 256 * b)]
+            else:
+                t = first + b // 2
+                if b % 2 == 0:
+                    a_codes[e, t] = work.tile([P, PASSES * P], U32, name="a_codes", bufs=6, align_bytes=64)
+                    a_scales[e, t] = work.tile([P, PASSES * P], U8, name="a_scales", bufs=6, align_bytes=64)
+                codes, scales = a_codes[e, t], a_scales[e, t]
+                spans = [slice(256 * (b % 2), 256 * (b % 2 + 1))]
+            width = 1024 // len(spans)
+            for n, span in enumerate(spans):
+                nc.vector.quantize_mx(
+                    out=codes[:, span].bitcast(FP8X4),
+                    scales=scales[:, span],
+                    in_=grouped[s, b][:, width * n : width * (n + 1)],
+                )
+
+        def multiply(e, ts, cols):
+            width = cols.stop - cols.start
+            bank = psum.tile([P, S], F32, name="bank")
+            for n, t in enumerate(ts):
+                for g in range(PASSES):
+                    span = x_span(e, g, cols)
+                    nc.tensor.matmul_mx(
+                        out=bank[:, width * n : width * (n + 1)],
+                        lhsT=a_codes[e, t][:, P * g : P * (g + 1)].bitcast(FP8X4),
+                        lhsT_scale=a_scales[e, t][:, P * g : P * (g + 1)],
+                        rhs=x_codes[e][:, span].bitcast(FP8X4),
+                        rhs_scale=x_scales[e][:, span],
+                        start=(g == 0),
+                        stop=(g == PASSES - 1),
                     )
-                return
-            t = 2 * h + b // 2
-            if b % 2 == (0 if s in SPLIT_Q else 1):
-                a_codes[e, t] = work.tile([P, PASSES * P], U32, name="a_codes", bufs=5, align_bytes=64)
-                a_scales[e, t] = work.tile([P, PASSES * P], U8, name="a_scales", bufs=5, align_bytes=64)
-            if s in SPLIT_Q:
-                cols = slice(256 * (b % 2), 256 * (b % 2 + 1))
-                nc.vector.quantize_mx(
-                    out=a_codes[e, t][:, cols].bitcast(FP8X4),
-                    scales=a_scales[e, t][:, cols],
-                    in_=grouped[s, b // 2][:, b % 2, :],
-                )
-            elif b % 2 == 1:
-                nc.vector.quantize_mx(
-                    out=a_codes[e, t][:].bitcast(FP8X4),
-                    scales=a_scales[e, t][:],
-                    in_=grouped[s, b // 2][:].rearrange("p n c -> p (n c)"),
-                )
-
-        def group_items(m):
-            e, n = divmod(m, 4)
-            if n < 2:
-                return [(e, t, slice(256 * n, 256 * (n + 1))) for t in range(2)]
-            return [(e, n, slice(0, 256)), (e, n, slice(256, 512))]
-
-        def finished_rows(m):
-            e, n = divmod(m, 4)
-            return [[], [(e, 0), (e, 1)], [(e, 2)], [(e, 3)]][n]
-
-        def multiply(e, t, cols, key, tag, passes=range(PASSES)):
-            if key not in acc:
-                acc[key] = psum.tile([P, S], F32, name=tag, bufs=8 - T_BANKS if tag == "acc" else T_BANKS)
-            h = cols.start // 256
-            window = slice(cols.start - 256 * h, cols.stop - 256 * h)
-            for g in passes:
-                nc.tensor.matmul_mx(
-                    out=acc[key][:, cols],
-                    lhsT=a_codes[e, t][:, P * g : P * (g + 1)].bitcast(FP8X4),
-                    lhsT_scale=a_scales[e, t][:, P * g : P * (g + 1)],
-                    rhs=x_codes[e][:, h, g, window].bitcast(FP8X4),
-                    rhs_scale=x_scales[e][:, h, g, window],
-                    start=(g == 0),
-                    stop=(g == PASSES - 1),
-                )
-
-        def scale_out(e, t, cols, key):
             if e not in y32:
-                y32[e] = work.tile([P, 4, S], F32, name="y32", bufs=E)
-            nc.scalar.activation(out=y32[e][:, t, cols], in_=acc[key][:, cols], func=COPY, scale=factor[:, t, e : e + 1])
+                y32[e] = work.tile([P, 4, S], F32, name="y32", bufs=3)
+            for n, t in enumerate(ts):
+                src = bank[:, width * n : width * (n + 1)]
+                if cols.start == 384 and t in TAIL_V:
+                    nc.vector.tensor_scalar(
+                        out=y32[e][:, t, cols], in0=src, scalar1=factor[:, t, e : e + 1], scalar2=None, op0=MULT
+                    )
+                else:
+                    nc.scalar.activation(out=y32[e][:, t, cols], in_=src, func=COPY, scale=factor[:, t, e : e + 1])
 
         def round_y(e, cols):
             if cols.start == 0:
                 y16[e] = work.tile([P, S, 4], BF16, name="y16", align_bytes=64)
-            if e == E - 1 and cols.start in S_ROUND:
-                nc.scalar.copy(out=y16[e][:, cols, :], in_=y32[e][:, :, cols].rearrange("p t s -> p s t"))
-                return
             nc.vector.tensor_copy(out=y16[e][:, cols, :], in_=y32[e][:, :, cols].rearrange("p t s -> p s t"))
 
         def quantise_y(e, cols):
@@ -231,178 +208,108 @@ def tile_lora_down_scaled_rank_planes_g2_kernel(tc, x, a_down, gain, alpha, out_
                 scales=y_scales[:, span],
                 in_=y16[e][:, cols, :].rearrange("p s t -> p (s t)"),
             )
+            if e == last_e and cols.start == 0:
+                return
+            if e == last_e and cols.start == 256:
+                span = slice(S * e, span.stop)
+            nc.sync.dma_start(out=words_out[:, span], in_=y_codes[:, span].bitcast(I32))
+            if e == 1:
+                store_scales(slice(0, S * 2), [nc.sync] * 4)
 
-        def store_y(e, ts, cols=slice(0, S)):
+        def store_y(e, ts, cols):
             rows = out_0[e].rearrange("(p t) s -> p t s", t=4)
             nc.sync.dma_start(out=rows[:, ts, cols], in_=y32[e][:, ts, cols])
 
-        def store_words(span):
-            nc.sync.dma_start(out=words_out[:, span], in_=y_codes[:, span].bitcast(I32))
-
-        def store_scales(span, engine):
+        def store_scales(span, engines):
             for q in range(4):
-                engine.dma_start(
+                engines[q].dma_start(
                     out=out_2[0, 4 * q : 4 * q + 4, span].bitcast(I32),
                     in_=y_scales[32 * q : 32 * q + 4, span].bitcast(I32),
                 )
 
-        whole = slice(0, S)
-        for s in range(RAW_BUFS):
-            load(s)
-        nc.scalar.dma_start(out=gain_sb[:], in_=gain)
+        for s in range(SINGLE + RAW_BUFS):
+            if s <= last:
+                load(s)
         with nc.allow_non_contiguous_dma(reason="one alpha to a partition"):
             nc.scalar.dma_start(out=alpha_sb[:], in_=alpha.rearrange("(e o) -> e o", o=1))
+        nc.scalar.dma_start(out=gain_sb[:], in_=gain)
         make_identity(nc, ident[:])
-        nc.vector.memset(warm[:], 0.0)
-        if WARM:
-            zeros = keep.tile([P, 4 * S], BF16, name="zeros", align_bytes=64)
-            zero_codes = keep.tile([P, S], U32, name="zero_codes", align_bytes=64)
-            zero_scales = keep.tile([P, S], U8, name="zero_scales", align_bytes=64)
-            spare = psum.tile([P, S], F32, name="acc", bufs=8 - T_BANKS)
-            nc.vector.memset(zeros[:].bitcast(I32), 0)
         nc.vector.memset(factor_rows[:], 0.0)
-        if WARM:
-            nc.vector.quantize_mx(out=zero_codes[:].bitcast(FP8X4), scales=zero_scales[:], in_=zeros[:])
+        nc.scalar.activation(out=alpha_over_rank[:], in_=alpha_sb[:], func=COPY, scale=1.0 / R)
 
-        def idle_pass():
-            nc.tensor.matmul_mx(
-                out=spare[:],
-                lhsT=zero_codes[:, :P].bitcast(FP8X4),
-                lhsT_scale=zero_scales[:, :P],
-                rhs=zero_codes[:].bitcast(FP8X4),
-                rhs_scale=zero_scales[:],
-                start=True,
-                stop=True,
+        def make_factor():
+            nc.vector.tensor_scalar(
+                out=factor_rows[0:E],
+                in0=gain_sb[:].rearrange("e (p t) -> e t p", t=4),
+                scalar1=alpha_over_rank[:],
+                scalar2=None,
+                op0=MULT,
             )
 
-        for n in range(WARM):
-            idle_pass()
-        nc.scalar.activation(out=warm[:], in_=warm[:], func=COPY)
-        nc.vector.tensor_scalar(
-            out=factor_rows[0:E, :], in0=gain_sb[:], scalar1=alpha_sb[:], scalar2=1.0 / R, op0=MULT, op1=MULT
-        )
-
         def turn_factor():
-            factor_bank = psum.tile([P, 4, P], F32, name="acc", bufs=8 - T_BANKS)
+            factor_bank = psum.tile([P, 4, P], F32, name="bank")
             for t in range(4):
-                nc.tensor.transpose(factor_bank[:, t, :], factor_rows[:, t::4], ident[:])
+                nc.tensor.transpose(factor_bank[:, t, :], factor_rows[:, t, :], ident[:])
             nc.scalar.copy(out=factor[:], in_=factor_bank[:, :, 0:E])
 
-        if FACTOR_AT < 0:
-            turn_factor()
-        save_second(0, 0)
-        gather_first(0, 0)
-        save_second(0, 1)
-        gather_first(0, 1)
+        sort(0)
 
-        last = len(steps) - 1
-        quantised = [0]
-
-        def quantise_until(n):
-            while quantised[0] < n:
-                quantise(*divmod(quantised[0], 4))
-                quantised[0] += 1
-
-        pending, todo, late = [], [], None
-        for s in range(len(steps)):
-            for b in range(4):
-                transposes(s, b)
-                for at in KEEP:
-                    if WARM and at == (s, b):
-                        idle_pass()
-            if s + RAW_BUFS <= last:
-                load(s + RAW_BUFS)
-            for b in range(4):
-                for m in pending:
-                    for n, (e, t) in enumerate(finished_rows(m)):
-                        if b == (ACC_POS, ACC_POS2)[n]:
-                            scale_out(e, t, whole, (e, t))
-                if (s, b) not in V_BANKS:
-                    empty_bank(s, b)
-            if s == FACTOR_AT:
-                turn_factor()
-            finished = [m // 4 for m in pending if m % 4 == 3]
-            pending = [m for m in range(14) if MM_AFTER[m] == s]
-            for e in finished:
-                todo = [(e, 1), (e, 2)] if WHOLE_ROUND else [(e, 0), (e, 1), (e, 2)]
-            order = VORD_H if s < HEAD else (VORD_L if s == last else (VORD_X if steps[s][0] == "x" else VORD_A))
-            lag = QLAG_H if s < HEAD else QLAG
-            for item in order.split():
-                if item[0] == "s":
-                    save_second(s + 1, int(item[1]))
-                elif item[0] == "g":
-                    gather_first(s + 1, int(item[1]))
-                elif item[0] == "e":
-                    for b in range(4):
-                        if (s, b) in V_BANKS:
-                            empty_bank(s, b)
-                elif item[0] == "q":
-                    quantise_until(4 * s + "abcd".index(item[1]) - lag + 1)
-                else:
-                    for n in range(2 if s == last else 1):
-                        if todo and todo[0][1] < 2:
-                            e, half = todo[0]
-                            round_y(e, whole if WHOLE_ROUND else slice(256 * half, 256 * (half + 1)))
-                            todo = todo[1:]
-                        elif todo and s != last:
-                            late = todo[0][0]
-                            todo = []
-            if s == last and todo:
-                late = todo[0][0]
-            if late is not None:
-                quantise_y(late, whole)
-            for m in pending:
-                need = [4 * (m // 4) * 4 + 8, 4 * (m // 4) * 4 + 12, 4 * (m // 4) * 4 + 14, 4 * (m // 4) * 4 + 16][m % 4]
-                quantise_until(need)
-                for e, t, cols in group_items(m):
-                    multiply(e, t, cols, (e, t), "acc")
-            for e in finished:
-                store_y(e, slice(0, 4))
-            if late is not None:
-                store_words(slice(S * late, S * (late + 1)))
-                if late == E - 2:
-                    store_scales(slice(0, S * (E - 1)), nc.sync)
-                late = None
-
-        quantise_until(4 * len(steps))
-        m = 13
-        e = E - 1
-        for t in range(2):
-            scale_out(e, t, whole, (e, t))
-        store_y(e, slice(0, 2))
-        parts = [slice(0, 256), slice(256, 384), slice(384, 512)] if TAILQ else [slice(0, 256), slice(256, 512)]
-        if TAIL == 0:
-            for n, cols in enumerate(parts):
-                if PAIR:
-                    pair = psum.tile([P, 2, S], F32, name="bank", bufs=T_BANKS // 2)
-                    acc[e, 2, n], acc[e, 3, n] = pair[:, 0, :], pair[:, 1, :]
-                for t in (2, 3):
-                    multiply(e, t, cols, (e, t, n), "bank")
-            for n, cols in enumerate(parts):
-                for t in (2, 3):
-                    scale_out(e, t, cols, (e, t, n))
+        s = 0
+        held, rounding, quantising, coming = [], [], [], []
+        for r, (run, products) in enumerate(runs):
+            banks = [(s + n, b) for n, unit in enumerate(run) for b in range(2 * unit[3])]
+            s += len(run)
+            while coming:
+                sort(coming.pop(0))
+            coming = list(range(s, s + len(runs[r + 1][0]))) if r + 1 < len(runs) else []
+            if len(banks) == 2:
+                sort(coming.pop(0))
+            if r == 0:
+                make_factor()
+            for n, (a, b) in enumerate(banks):
+                turn(a, b, (r, n) in V_BANKS)
                 if n == 0:
-                    store_y(e, slice(2, 4), cols)
-            store_y(e, slice(2, 4), slice(256, 512))
-        else:
-            for h in range(2):
-                multiply(e, 2, slice(256 * h, 256 * (h + 1)), (e, 2), "bank")
-            for passes in (range(2), range(2, 4)):
-                for n, cols in enumerate(parts):
-                    multiply(e, 3, cols, (e, 3, n), "bank", passes)
-            scale_out(e, 2, whole, (e, 2))
-            store_y(e, slice(2, 3))
-            for n, cols in enumerate(parts):
-                scale_out(e, 3, cols, (e, 3, n))
-            store_y(e, slice(3, 4))
-        round_y(e, parts[0])
-        round_y(e, parts[1])
-        quantise_y(e, parts[0])
-        store_words(slice(S * e, S * e + 256))
-        if TAILQ:
-            round_y(e, parts[2])
-        quantise_y(e, parts[1])
-        if TAILQ:
-            quantise_y(e, parts[2])
-        store_words(slice(S * e + 256, S * E))
-        store_scales(slice(S * e, S * E), nc.scalar)
+                    for item in held:
+                        quantise(*item)
+                    held = []
+            if r == FACTOR_AT:
+                turn_factor()
+            for a in range(s - len(run), s):
+                if units[a][3] == 2 and a + RAW_BUFS <= last:
+                    load(a + RAW_BUFS)
+            if quantising:
+                quantise_y(*quantising.pop(0))
+            if -1 in SORT_AT[r]:
+                sort(coming.pop(0))
+            for n, (a, b) in enumerate(banks):
+                if n < len(banks) - HOLD[r]:
+                    quantise(a, b)
+                else:
+                    held.append((a, b))
+                if coming and n in SORT_AT[r]:
+                    sort(coming.pop(0))
+                if rounding:
+                    item = rounding.pop(0)
+                    round_y(*item)
+                    if not rounding:
+                        quantising.append((item[0], whole))
+            for e, ts, cols in products:
+                multiply(e, ts, cols)
+                if e == last_e:
+                    if cols.start == 0:
+                        store_y(e, slice(ts[0], ts[-1] + 1), cols)
+                    elif ts[-1] == 3:
+                        store_y(e, slice(0, 4), cols)
+                    if quantising:
+                        quantise_y(*quantising.pop(0))
+                elif ts[-1] == 3:
+                    store_y(e, slice(0, 4), whole)
+                    rounding = [(e, slice(c, c + ROUND_COLS)) for c in range(0, S, ROUND_COLS)]
+        parts = [first_half, slice(256, 384), slice(384, 512)]
+        round_y(last_e, parts[0])
+        round_y(last_e, parts[1])
+        quantise_y(last_e, parts[0])
+        quantise_y(last_e, parts[1])
+        round_y(last_e, parts[2])
+        quantise_y(last_e, parts[2])
+        store_scales(slice(S * 2, S * E), [nc.scalar, nc.scalar, nc.sync, nc.sync])

@@ -26,10 +26,18 @@ SINGLE = 8
 ROUND_COLS = 128
 TAIL_V = ()
 FACTOR_AT = 2
-V_BANKS = ((8, 0), (9, 0), (10, 0), (11, 0), (12, 0), (13, 0), (14, 0))
-HOLD = [2] * 8 + [1, 1, 0, 1, 0, 1, 0]
-SORT_AT = [()] * 8 + [(-1,), (-1, 2), (3, 5), (1, 4), (3, 5), (1, 4), ()]
+R7 = "hsqqs"
+R8 = "eqqsqqqqqsq"
+R9 = "ehqrqrqrqsrqqsqq"
+R11 = "eyqqsqqqsqq"
+R12 = "ehqrqrqrqsrqqsqq"
+R13 = "eyqqsqqqsqq"
+R14 = "ehqrqrqrqrqqyqq"
 GROUPED = 10
+LONE = 2
+WIDE = 2
+ORDER = (3, 2, 1, 0)
+BACK_FROM = 2
 
 
 def tile_lora_down_scaled_rank_planes_g2_kernel(tc, x, a_down, gain, alpha, out_0, out_1, out_2):
@@ -37,27 +45,27 @@ def tile_lora_down_scaled_rank_planes_g2_kernel(tc, x, a_down, gain, alpha, out_
     last_e = E - 1
     first_half, second_half, whole = slice(0, 256), slice(256, 512), slice(0, S)
     runs = [
-        ([("a", 0, 0, 1)], []),
-        ([("x", 0, 0, 1)], []),
-        ([("x", 0, 1, 1)], []),
-        ([("a", 0, 1, 1)], []),
-        ([("x", 0, 2, 1)], [(0, (0,), first_half)]),
-        ([("x", 0, 3, 1)], [(0, (1,), first_half)]),
-        ([("a", 0, 2, 1)], []),
-        ([("a", 0, 3, 1)], [(0, (0, 1), second_half)]),
-        ([("x", 1, 0, 2)], [(0, (2,), whole)]),
-        ([("x", 1, 2, 2)], [(0, (3,), whole)]),
-        ([("a", 1, 0, 2), ("a", 1, 2, 2)], [(1, (0,), whole), (1, (1,), whole)]),
-        ([("x", 2, 0, 2), ("x", 2, 2, 2)], [(1, (2,), whole), (1, (3,), whole)]),
-        ([("a", 2, 0, 2), ("a", 2, 2, 2)], [(2, (0,), whole), (2, (1,), whole)]),
-        ([("a", 3, 0, 2), ("x", 3, 0, 2)], [(2, (2,), whole), (2, (3,), whole)]),
+        ([("a", 0, 0, 1)], [], "sf"),
+        ([("x", 0, 0, 1)], [], "sh"),
+        ([("x", 0, 1, 1)], [], "sh"),
+        ([("a", 0, 1, 1)], [], "sh"),
+        ([("x", 0, 2, 1)], [(0, (0,), first_half)], "sh"),
+        ([("x", 0, 3, 1)], [(0, (1,), first_half)], "sh"),
+        ([("a", 0, 2, 1)], [], "sh"),
+        ([("a", 0, 3, 1)], [(0, (0, 1), second_half), (0, (2,), whole)], R7),
+        ([("x", 1, 0, 2), ("x", 1, 2, 2)], [(0, (3,), whole)], R8),
+        ([("a", 1, 0, 2), ("a", 1, 2, 2)], [(1, (0,), whole), (1, (1,), whole)], R9),
+        ([("x", 2, 0, 2), ("x", 2, 2, 2)], [(1, (2,), whole), (1, (3,), whole)], R11),
+        ([("a", 2, 0, 2), ("a", 2, 2, 2)], [(2, (0,), whole), (2, (1,), whole)], R12),
+        ([("a", 3, 0, 2), ("x", 3, 0, 2)], [(2, (2,), whole), (2, (3,), whole)], R13),
         (
             [("a", 3, 2, 2), ("x", 3, 2, 2)],
-            [(3, (0, 1), first_half), (3, (2, 3), first_half), (3, (0, 1, 2, 3), slice(256, 384))]
+            [(3, (0, 1), first_half), (3, (2, 3), first_half), (3, (0, 1), slice(256, 384)), (3, (2, 3), slice(256, 384))]
             + [(3, ts, slice(384, 512)) for ts in TAIL_TS],
+            R14,
         ),
     ]
-    units = [unit for run, products in runs for unit in run]
+    units = [unit for run, products, order in runs for unit in run]
     last = len(units) - 1
 
     words_out = out_1[0].rearrange("p m t -> p (m t)").bitcast(I32)
@@ -65,7 +73,7 @@ def tile_lora_down_scaled_rank_planes_g2_kernel(tc, x, a_down, gain, alpha, out_
     with ExitStack() as ctx:
         keep = ctx.enter_context(tc.tile_pool(name="keep", bufs=1))
         work = ctx.enter_context(tc.tile_pool(name="work", bufs=2))
-        psum = ctx.enter_context(tc.psum_pool(name="psum", bufs=8))
+        psum = ctx.enter_context(tc.psum_pool(name="psum", bufs=1))
         ctx.enter_context(tc.manual_schedule())
 
         ident = keep.tile([P, P], F32, name="ident")
@@ -75,10 +83,17 @@ def tile_lora_down_scaled_rank_planes_g2_kernel(tc, x, a_down, gain, alpha, out_
         factor_rows = keep.tile([P, 4, P], F32, name="factor_rows")
         factor = keep.tile([P, 4, E], F32, name="factor")
         y_codes = keep.tile([P, E * S], U32, name="y_codes", align_bytes=64)
-        y_scales = keep.tile([P, E * S], U8, name="y_scales", align_bytes=64)
+        y_scales = keep.tile([P, S], U8, name="y_scales", align_bytes=64)
 
         raw, windows, grouped = {}, {}, {}
         x_codes, x_scales, a_codes, a_scales, y32, y16 = {}, {}, {}, {}, {}, {}
+
+        taken = [0]
+
+        def next_banks(count):
+            first = taken[0] + taken[0] % count
+            taken[0] = first + count
+            return psum.tile([P, count, S], F32, name="banks%d" % first, offset=2048 * (first % 8))
 
         def load(s):
             kind, e, first, count = units[s]
@@ -120,19 +135,19 @@ def tile_lora_down_scaled_rank_planes_g2_kernel(tc, x, a_down, gain, alpha, out_
         def by_pass(s):
             return units[s][0] == "x" and units[s][3] == 2 and s != last
 
-        def turn(s, b, on_vector):
-            bank = psum.tile([P, 2, 2, P], F32, name="bank")
-            items = [(0, b), (1, b)] if by_pass(s) else [(b // 2, 2 * (b % 2)), (b // 2, 2 * (b % 2) + 1)]
-            for n, (j, g) in enumerate(items):
-                for u in range(2):
-                    nc.tensor.transpose(bank[:, n, u, :], windows[s, j][u][:, P * g : P * (g + 1)], ident[:])
-            grouped[s, b] = work.tile([P, 4 * 2 * P], BF16, name="grouped", bufs=GROUPED, align_bytes=64)
-            dst = grouped[s, b][:].bitcast(F32).rearrange("p (n r u) -> p n r u", n=2, u=2)
-            src = bank[:].rearrange("p n u r -> p n r u")
-            if on_vector:
-                nc.vector.tensor_copy(out=dst, in_=src)
-            else:
-                nc.scalar.copy(out=dst, in_=src)
+        def turn(s, first, count):
+            tile = next_banks(count)
+            moves = []
+            for b in range(first, first + count):
+                bank = tile[:, b - first, :].rearrange("p (n u r) -> p n u r", n=2, u=2)
+                items = [(0, b), (1, b)] if by_pass(s) else [(b // 2, 2 * (b % 2)), (b // 2, 2 * (b % 2) + 1)]
+                for n, (j, g) in enumerate(items):
+                    for u in range(2):
+                        nc.tensor.transpose(bank[:, n, u, :], windows[s, j][u][:, P * g : P * (g + 1)], ident[:])
+                grouped[s, b] = work.tile([P, 4 * 2 * P], BF16, name="grouped", bufs=GROUPED, align_bytes=64)
+                dst = grouped[s, b][:].bitcast(F32).rearrange("p (n r u) -> p n r u", n=2, u=2)
+                moves.append((dst, bank.rearrange("p n u r -> p n r u")))
+            return moves
 
         def x_span(e, g, cols):
             if e != last_e:
@@ -172,9 +187,10 @@ def tile_lora_down_scaled_rank_planes_g2_kernel(tc, x, a_down, gain, alpha, out_
 
         def multiply(e, ts, cols):
             width = cols.stop - cols.start
-            bank = psum.tile([P, S], F32, name="bank")
+            bank = next_banks(1)[:, 0, :]
             for n, t in enumerate(ts):
-                for g in range(PASSES):
+                order = ORDER if e >= BACK_FROM else (0, 1, 2, 3)
+                for g in order:
                     span = x_span(e, g, cols)
                     nc.tensor.matmul_mx(
                         out=bank[:, width * n : width * (n + 1)],
@@ -182,8 +198,8 @@ def tile_lora_down_scaled_rank_planes_g2_kernel(tc, x, a_down, gain, alpha, out_
                         lhsT_scale=a_scales[e, t][:, P * g : P * (g + 1)],
                         rhs=x_codes[e][:, span].bitcast(FP8X4),
                         rhs_scale=x_scales[e][:, span],
-                        start=(g == 0),
-                        stop=(g == PASSES - 1),
+                        start=(g == order[0]),
+                        stop=(g == order[-1]),
                     )
             if e not in y32:
                 y32[e] = work.tile([P, 4, S], F32, name="y32", bufs=3)
@@ -199,32 +215,32 @@ def tile_lora_down_scaled_rank_planes_g2_kernel(tc, x, a_down, gain, alpha, out_
         def round_y(e, cols):
             if cols.start == 0:
                 y16[e] = work.tile([P, S, 4], BF16, name="y16", align_bytes=64)
-            nc.vector.tensor_copy(out=y16[e][:, cols, :], in_=y32[e][:, :, cols].rearrange("p t s -> p s t"))
+            nc.vector.tensor_copy(
+                out=y16[e][:, cols, :].rearrange("p (c i) t -> p c t i", i=4),
+                in_=y32[e][:, :, cols].rearrange("p t (c i) -> p c t i", i=4),
+            )
 
         def quantise_y(e, cols):
             span = slice(S * e + cols.start, S * e + cols.stop)
             nc.vector.quantize_mx(
                 out=y_codes[:, span].bitcast(FP8X4),
-                scales=y_scales[:, span],
+                scales=y_scales[4 * e :, cols],
                 in_=y16[e][:, cols, :].rearrange("p s t -> p (s t)"),
             )
-            if e == last_e and cols.start == 0:
-                return
-            if e == last_e and cols.start == 256:
-                span = slice(S * e, span.stop)
+
+        def store_words(e, cols):
+            span = slice(S * e + cols.start, S * e + cols.stop)
             nc.sync.dma_start(out=words_out[:, span], in_=y_codes[:, span].bitcast(I32))
-            if e == 1:
-                store_scales(slice(0, S * 2), [nc.sync] * 4)
 
         def store_y(e, ts, cols):
             rows = out_0[e].rearrange("(p t) s -> p t s", t=4)
             nc.sync.dma_start(out=rows[:, ts, cols], in_=y32[e][:, ts, cols])
 
-        def store_scales(span, engines):
+        def store_scales(engines):
             for q in range(4):
                 engines[q].dma_start(
-                    out=out_2[0, 4 * q : 4 * q + 4, span].bitcast(I32),
-                    in_=y_scales[32 * q : 32 * q + 4, span].bitcast(I32),
+                    out=out_2[0, 4 * q : 4 * q + 4, :].bitcast(I32).rearrange("r (e s) -> e r s", e=E),
+                    in_=y_scales[32 * q : 32 * q + 4 * E, :].bitcast(I32),
                 )
 
         for s in range(SINGLE + RAW_BUFS):
@@ -247,52 +263,59 @@ def tile_lora_down_scaled_rank_planes_g2_kernel(tc, x, a_down, gain, alpha, out_
             )
 
         def turn_factor():
-            factor_bank = psum.tile([P, 4, P], F32, name="bank")
+            factor_bank = next_banks(1)[:, 0, :].rearrange("p (t r) -> p t r", t=4)
             for t in range(4):
                 nc.tensor.transpose(factor_bank[:, t, :], factor_rows[:, t, :], ident[:])
             nc.scalar.copy(out=factor[:], in_=factor_bank[:, :, 0:E])
 
         sort(0)
 
-        s = 0
-        held, rounding, quantising, coming = [], [], [], []
-        for r, (run, products) in enumerate(runs):
+        s, unsorted = 0, 1
+        held, rounding, quantising = [], [], []
+        for r, (run, products, order) in enumerate(runs):
             banks = [(s + n, b) for n, unit in enumerate(run) for b in range(2 * unit[3])]
             s += len(run)
-            while coming:
-                sort(coming.pop(0))
-            coming = list(range(s, s + len(runs[r + 1][0]))) if r + 1 < len(runs) else []
-            if len(banks) == 2:
-                sort(coming.pop(0))
-            if r == 0:
-                make_factor()
+            filled = []
+            taken[0] += taken[0] % 2
             for n, (a, b) in enumerate(banks):
-                turn(a, b, (r, n) in V_BANKS)
-                if n == 0:
-                    for item in held:
-                        quantise(*item)
-                    held = []
+                count = 1 if n < LONE or len(banks) < 8 else WIDE
+                if count > 1 and (n - LONE) % count:
+                    continue
+                for dst, src in turn(a, b, min(count, 4 - b)):
+                    if "e" in order and not filled:
+                        filled.append((dst, src))
+                    else:
+                        nc.scalar.copy(out=dst, in_=src)
             if r == FACTOR_AT:
                 turn_factor()
             for a in range(s - len(run), s):
                 if units[a][3] == 2 and a + RAW_BUFS <= last:
                     load(a + RAW_BUFS)
-            if quantising:
-                quantise_y(*quantising.pop(0))
-            if -1 in SORT_AT[r]:
-                sort(coming.pop(0))
-            for n, (a, b) in enumerate(banks):
-                if n < len(banks) - HOLD[r]:
-                    quantise(a, b)
-                else:
-                    held.append((a, b))
-                if coming and n in SORT_AT[r]:
-                    sort(coming.pop(0))
-                if rounding:
-                    item = rounding.pop(0)
-                    round_y(*item)
+            if len(rounding) * ROUND_COLS == S:
+                store_y(rounding[0][0], slice(0, 4), whole)
+            for item in order:
+                if item == "e":
+                    nc.vector.tensor_copy(out=filled[0][0], in_=filled[0][1])
+                elif item == "f":
+                    make_factor()
+                elif item == "h":
+                    while held:
+                        quantise(*held.pop(0))
+                elif item == "q":
+                    quantise(*banks.pop(0))
+                elif item == "s":
+                    sort(unsorted)
+                    unsorted += 1
+                elif item == "r":
+                    e, cols = rounding.pop(0)
+                    round_y(e, cols)
                     if not rounding:
-                        quantising.append((item[0], whole))
+                        quantising.append(e)
+                else:
+                    e = quantising.pop(0)
+                    quantise_y(e, whole)
+                    store_words(e, whole)
+            held += banks
             for e, ts, cols in products:
                 multiply(e, ts, cols)
                 if e == last_e:
@@ -300,16 +323,12 @@ def tile_lora_down_scaled_rank_planes_g2_kernel(tc, x, a_down, gain, alpha, out_
                         store_y(e, slice(ts[0], ts[-1] + 1), cols)
                     elif ts[-1] == 3:
                         store_y(e, slice(0, 4), cols)
-                    if quantising:
-                        quantise_y(*quantising.pop(0))
+                    if ts[-1] == 3:
+                        if cols.start == 256:
+                            store_words(e, first_half)
+                        round_y(e, cols)
+                        quantise_y(e, cols)
                 elif ts[-1] == 3:
-                    store_y(e, slice(0, 4), whole)
                     rounding = [(e, slice(c, c + ROUND_COLS)) for c in range(0, S, ROUND_COLS)]
-        parts = [first_half, slice(256, 384), slice(384, 512)]
-        round_y(last_e, parts[0])
-        round_y(last_e, parts[1])
-        quantise_y(last_e, parts[0])
-        quantise_y(last_e, parts[1])
-        round_y(last_e, parts[2])
-        quantise_y(last_e, parts[2])
-        store_scales(slice(S * 2, S * E), [nc.scalar, nc.scalar, nc.sync, nc.sync])
+        store_words(last_e, second_half)
+        store_scales([nc.scalar, nc.scalar, nc.sync, nc.sync])

@@ -34,10 +34,11 @@ R12 = "ehqrqrqrqsrqqsqq"
 R13 = "eyqqsqqqsqq"
 R14 = "ehqrqrqrqrqqyqq"
 GROUPED = 10
+PGROUP = 2
 LONE = 2
 WIDE = 2
 ORDER = (3, 2, 1, 0)
-BACK_FROM = 2
+FORWARD = 1
 
 
 def tile_lora_down_scaled_rank_planes_g2_kernel(tc, x, a_down, gain, alpha, out_0, out_1, out_2):
@@ -55,9 +56,9 @@ def tile_lora_down_scaled_rank_planes_g2_kernel(tc, x, a_down, gain, alpha, out_
         ([("a", 0, 3, 1)], [(0, (0, 1), second_half), (0, (2,), whole)], R7),
         ([("x", 1, 0, 2), ("x", 1, 2, 2)], [(0, (3,), whole)], R8),
         ([("a", 1, 0, 2), ("a", 1, 2, 2)], [(1, (0,), whole), (1, (1,), whole)], R9),
-        ([("x", 2, 0, 2), ("x", 2, 2, 2)], [(1, (2,), whole), (1, (3,), whole)], R11),
+        ([("x", 2, 0, 2), ("x", 2, 2, 2)], [(1, (3,), whole), (1, (2,), whole)], R11),
         ([("a", 2, 0, 2), ("a", 2, 2, 2)], [(2, (0,), whole), (2, (1,), whole)], R12),
-        ([("a", 3, 0, 2), ("x", 3, 0, 2)], [(2, (2,), whole), (2, (3,), whole)], R13),
+        ([("a", 3, 0, 2), ("x", 3, 0, 2)], [(2, (3,), whole), (2, (2,), whole)], R13),
         (
             [("a", 3, 2, 2), ("x", 3, 2, 2)],
             [(3, (0, 1), first_half), (3, (2, 3), first_half), (3, (0, 1), slice(256, 384)), (3, (2, 3), slice(256, 384))]
@@ -88,12 +89,16 @@ def tile_lora_down_scaled_rank_planes_g2_kernel(tc, x, a_down, gain, alpha, out_
         raw, windows, grouped = {}, {}, {}
         x_codes, x_scales, a_codes, a_scales, y32, y16 = {}, {}, {}, {}, {}, {}
 
-        taken = [0]
+        free, made = list(range(8)), [0]
 
-        def next_banks(count):
-            first = taken[0] + taken[0] % count
-            taken[0] = first + count
-            return psum.tile([P, count, S], F32, name="banks%d" % first, offset=2048 * (first % 8))
+        def take(count):
+            chosen = free[:count][::-1]
+            free[:] = free[count:] + chosen
+            tiles = []
+            for place in chosen:
+                made[0] += 1
+                tiles.append(psum.tile([P, S], F32, name="bank%d" % made[0], offset=2048 * place))
+            return tiles
 
         def load(s):
             kind, e, first, count = units[s]
@@ -135,11 +140,10 @@ def tile_lora_down_scaled_rank_planes_g2_kernel(tc, x, a_down, gain, alpha, out_
         def by_pass(s):
             return units[s][0] == "x" and units[s][3] == 2 and s != last
 
-        def turn(s, first, count):
-            tile = next_banks(count)
+        def turn(s, first, count, tiles):
             moves = []
             for b in range(first, first + count):
-                bank = tile[:, b - first, :].rearrange("p (n u r) -> p n u r", n=2, u=2)
+                bank = tiles[b][:].rearrange("p (n u r) -> p n u r", n=2, u=2)
                 items = [(0, b), (1, b)] if by_pass(s) else [(b // 2, 2 * (b % 2)), (b // 2, 2 * (b % 2) + 1)]
                 for n, (j, g) in enumerate(items):
                     for u in range(2):
@@ -185,11 +189,10 @@ def tile_lora_down_scaled_rank_planes_g2_kernel(tc, x, a_down, gain, alpha, out_
                     in_=grouped[s, b][:, width * n : width * (n + 1)],
                 )
 
-        def multiply(e, ts, cols):
+        def multiply(e, ts, cols, bank):
             width = cols.stop - cols.start
-            bank = next_banks(1)[:, 0, :]
             for n, t in enumerate(ts):
-                order = ORDER if e >= BACK_FROM else (0, 1, 2, 3)
+                order = ORDER if e != FORWARD else (0, 1, 2, 3)
                 for g in order:
                     span = x_span(e, g, cols)
                     nc.tensor.matmul_mx(
@@ -263,7 +266,7 @@ def tile_lora_down_scaled_rank_planes_g2_kernel(tc, x, a_down, gain, alpha, out_
             )
 
         def turn_factor():
-            factor_bank = next_banks(1)[:, 0, :].rearrange("p (t r) -> p t r", t=4)
+            factor_bank = take(1)[0][:].rearrange("p (t r) -> p t r", t=4)
             for t in range(4):
                 nc.tensor.transpose(factor_bank[:, t, :], factor_rows[:, t, :], ident[:])
             nc.scalar.copy(out=factor[:], in_=factor_bank[:, :, 0:E])
@@ -276,12 +279,10 @@ def tile_lora_down_scaled_rank_planes_g2_kernel(tc, x, a_down, gain, alpha, out_
             banks = [(s + n, b) for n, unit in enumerate(run) for b in range(2 * unit[3])]
             s += len(run)
             filled = []
-            taken[0] += taken[0] % 2
             for n, (a, b) in enumerate(banks):
-                count = 1 if n < LONE or len(banks) < 8 else WIDE
-                if count > 1 and (n - LONE) % count:
-                    continue
-                for dst, src in turn(a, b, min(count, 4 - b)):
+                if b == 0:
+                    tiles = take(2 * units[a][3])
+                for dst, src in turn(a, b, 1, tiles):
                     if "e" in order and not filled:
                         filled.append((dst, src))
                     else:
@@ -316,8 +317,10 @@ def tile_lora_down_scaled_rank_planes_g2_kernel(tc, x, a_down, gain, alpha, out_
                     quantise_y(e, whole)
                     store_words(e, whole)
             held += banks
-            for e, ts, cols in products:
-                multiply(e, ts, cols)
+            for n, (e, ts, cols) in enumerate(products):
+                if n % PGROUP == 0:
+                    tiles = take(min(PGROUP, len(products) - n))
+                multiply(e, ts, cols, tiles[n % PGROUP])
                 if e == last_e:
                     if cols.start == 0:
                         store_y(e, slice(ts[0], ts[-1] + 1), cols)
@@ -328,7 +331,7 @@ def tile_lora_down_scaled_rank_planes_g2_kernel(tc, x, a_down, gain, alpha, out_
                             store_words(e, first_half)
                         round_y(e, cols)
                         quantise_y(e, cols)
-                elif ts[-1] == 3:
+                elif n == len(products) - 1 and ts[0] >= 2 and (e > 0 or ts[0] == 3):
                     rounding = [(e, slice(c, c + ROUND_COLS)) for c in range(0, S, ROUND_COLS)]
         store_words(last_e, second_half)
         store_scales([nc.scalar, nc.scalar, nc.sync, nc.sync])

@@ -18,8 +18,9 @@ COPY = mybir.ActivationFunctionType.Copy
 P = 128
 PASSES = 4
 HALF = 16
-FRONT = 32
-ROW = FRONT + D + 64
+FRONT = 128
+ROW = FRONT + D
+REACH = D // 2 + 2 * HALF
 RAW_BUFS = 10
 TAIL_TS = ((0,), (1,), (2,), (3,))
 SINGLE = 8
@@ -83,10 +84,10 @@ def tile_lora_down_scaled_rank_planes_g2_kernel(tc, x, a_down, gain, alpha, out_
         alpha_over_rank = keep.tile([E, 1], F32, name="alpha_over_rank")
         factor_rows = keep.tile([P, 4, P], F32, name="factor_rows")
         factor = keep.tile([P, 4, E], F32, name="factor")
-        y_codes = keep.tile([P, E * S], U32, name="y_codes", align_bytes=64)
-        y_scales = keep.tile([P, S], U8, name="y_scales", align_bytes=64)
+        y_codes = keep.tile([P, E * S], U32, name="y_codes", align_bytes=256)
+        y_scales = keep.tile([P, S], U8, name="y_scales", align_bytes=256)
 
-        raw, windows, grouped = {}, {}, {}
+        raw, flat, windows, grouped = {}, {}, {}, {}
         x_codes, x_scales, a_codes, a_scales, y32, y16 = {}, {}, {}, {}, {}, {}
 
         free, made = list(range(8)), [0]
@@ -107,15 +108,17 @@ def tile_lora_down_scaled_rank_planes_g2_kernel(tc, x, a_down, gain, alpha, out_
             else:
                 src = a_down[e].rearrange("(p t) k -> p t k", t=4)[:, first : first + count, :]
             if count == 1:
-                raw[s] = work.tile([P, D], BF16, name="lone", bufs=SINGLE, align_bytes=64)
+                raw[s] = work.tile([P, D], BF16, name="lone", bufs=SINGLE, align_bytes=256)
                 nc.sync.dma_start(out=raw[s][:], in_=src[:, 0, :])
             else:
-                raw[s] = work.tile([P, 2, ROW], BF16, name="raw", bufs=RAW_BUFS, align_bytes=64)
+                flat[s] = work.tile([P, 2 * ROW + FRONT], BF16, name="raw", bufs=RAW_BUFS, align_bytes=256)
+                raw[s] = flat[s][:, : 2 * ROW].rearrange("p (j k) -> p j k", j=2)
                 nc.sync.dma_start(out=raw[s][:, :, FRONT : FRONT + D], in_=src)
 
         def sort_pair(s):
             halves = raw[s][:, :, FRONT : FRONT + D].rearrange("p j (r b u i) -> p j b r u i", r=2, u=2, i=HALF)
-            span = raw[s][:, :, FRONT - HALF : FRONT - HALF + 2 * (D // 2 + 2 * HALF)]
+            rows = flat[s][:, FRONT - HALF : FRONT - HALF + 2 * ROW].rearrange("p (j k) -> p j k", j=2)
+            span = rows[:, :, : 2 * REACH]
             dst = span.rearrange("p j (r c i) -> p j c r i", r=2, i=HALF)[:, :, 0:64:2, :, :]
             nc.vector.tensor_copy(out=dst, in_=halves[:, :, :, ::-1, 1, :])
             for j in range(2):
@@ -205,7 +208,7 @@ def tile_lora_down_scaled_rank_planes_g2_kernel(tc, x, a_down, gain, alpha, out_
                         stop=(g == order[-1]),
                     )
             if e not in y32:
-                y32[e] = work.tile([P, 4, S], F32, name="y32", bufs=3)
+                y32[e] = work.tile([P, 4, S], F32, name="y32", bufs=3, align_bytes=256)
             for n, t in enumerate(ts):
                 src = bank[:, width * n : width * (n + 1)]
                 if cols.start == 384 and t in TAIL_V:

@@ -16,60 +16,55 @@ MULT = mybir.AluOpType.mult
 COPY = mybir.ActivationFunctionType.Copy
 
 P = 128
-PASSES = 4
+PASSES = D // 512
+SLOTS = 4
+BANKS = 8
+BANK_BYTES = 2048
+BANK_COLS = 256
 HALF = 16
-FRONT = 128
+ALIGN = 256
+FRONT = ALIGN // 2
 ROW = FRONT + D
 REACH = D // 2 + 2 * HALF
-RAW_BUFS = 10
-TAIL_TS = ((0,), (1,), (2,), (3,))
-SINGLE = 8
-ROUND_COLS = 128
-TAIL_V = ()
-FACTOR_AT = 2
-R7 = "hsqqs"
-R8 = "eqqsqqqqqsq"
-R9 = "ehqrqrqrqsrqqsqq"
-R11 = "eyqqsqqqsqq"
-R12 = "ehqrqrqrqsrqqsqq"
-R13 = "eyqqsqqqsqq"
-R14 = "ehqrqrqrqrqqyqq"
-GROUPED = 10
-PGROUP = 2
-LONE = 2
-WIDE = 2
-ORDER = (3, 2, 1, 0)
-FORWARD = 1
+PAIR_BUFS = 10
+SIDE_BUFS = 3
+TURNED_BUFS = 10
+A_BUFS = 6
+Y_BUFS = 3
+EARLY_SORT = 2
 
 
 def tile_lora_down_scaled_rank_planes_g2_kernel(tc, x, a_down, gain, alpha, out_0, out_1, out_2):
     nc = tc.nc
     last_e = E - 1
-    first_half, second_half, whole = slice(0, 256), slice(256, 512), slice(0, S)
-    runs = [
-        ([("a", 0, 0, 1)], [], "sf"),
-        ([("x", 0, 0, 1)], [], "sh"),
-        ([("x", 0, 1, 1)], [], "sh"),
-        ([("a", 0, 1, 1)], [], "sh"),
-        ([("x", 0, 2, 1)], [(0, (0,), first_half)], "sh"),
-        ([("x", 0, 3, 1)], [(0, (1,), first_half)], "sh"),
-        ([("a", 0, 2, 1)], [], "sh"),
-        ([("a", 0, 3, 1)], [(0, (0, 1), second_half), (0, (2,), whole)], R7),
-        ([("x", 1, 0, 2), ("x", 1, 2, 2)], [(0, (3,), whole)], R8),
-        ([("a", 1, 0, 2), ("a", 1, 2, 2)], [(1, (0,), whole), (1, (1,), whole)], R9),
-        ([("x", 2, 0, 2), ("x", 2, 2, 2)], [(1, (3,), whole), (1, (2,), whole)], R11),
-        ([("a", 2, 0, 2), ("a", 2, 2, 2)], [(2, (0,), whole), (2, (1,), whole)], R12),
-        ([("a", 3, 0, 2), ("x", 3, 0, 2)], [(2, (3,), whole), (2, (2,), whole)], R13),
-        (
-            [("a", 3, 2, 2), ("x", 3, 2, 2)],
-            [(3, (0, 1), first_half), (3, (2, 3), first_half), (3, (0, 1), slice(256, 384)), (3, (2, 3), slice(256, 384))]
-            + [(3, ts, slice(384, 512)) for ts in TAIL_TS],
-            R14,
-        ),
-    ]
-    units = [unit for run, products, order in runs for unit in run]
-    last = len(units) - 1
+    whole, low, high = slice(0, S), slice(0, S // 2), slice(S // 2, S)
+    third, fourth = slice(S // 2, S // 2 + P), slice(S // 2 + P, S)
 
+    head = [
+        ([("a", 0, 0, 1)], []),
+        ([("x", 0, 0, 1)], []),
+        ([("x", 0, 1, 1)], []),
+        ([("a", 0, 1, 1)], []),
+        ([("x", 0, 2, 1)], [(0, (0,), low)]),
+        ([("x", 0, 3, 1)], [(0, (1,), low)]),
+        ([("a", 0, 2, 1)], []),
+        ([("a", 0, 3, 1)], [(0, (0, 1), high), (0, (2,), whole)]),
+    ]
+    body = []
+    for e in range(1, last_e):
+        left_over = [(e - 1, (t,), whole) for t in ((3,) if e == 1 else (3, 2))]
+        body.append(([("x", e, 0, 2), ("x", e, 2, 2)], left_over))
+        body.append(([("a", e, 0, 2), ("a", e, 2, 2)], [(e, (0,), whole), (e, (1,), whole)]))
+    body.append(([("a", last_e, 0, 2), ("x", last_e, 0, 2)], [(last_e - 1, (t,), whole) for t in (3, 2)]))
+    body.append(
+        (
+            [("a", last_e, 2, 2), ("x", last_e, 2, 2)],
+            [(last_e, ts, cols) for cols in (low, third) for ts in ((0, 1), (2, 3))]
+            + [(last_e, (t,), fourth) for t in range(SLOTS)],
+        )
+    )
+    loads = [item for run, products in head + body for item in run]
+    last = len(loads) - 1
     words_out = out_1[0].rearrange("p m t -> p (m t)").bitcast(I32)
 
     with ExitStack() as ctx:
@@ -78,124 +73,117 @@ def tile_lora_down_scaled_rank_planes_g2_kernel(tc, x, a_down, gain, alpha, out_
         psum = ctx.enter_context(tc.psum_pool(name="psum", bufs=1))
         ctx.enter_context(tc.manual_schedule())
 
-        ident = keep.tile([P, P], F32, name="ident")
+        ident = keep.tile([P, P], F32, name="ident", align_bytes=ALIGN)
         gain_sb = keep.tile([E, R], BF16, name="gain_sb")
         alpha_sb = keep.tile([E, 1], BF16, name="alpha_sb")
         alpha_over_rank = keep.tile([E, 1], F32, name="alpha_over_rank")
-        factor_rows = keep.tile([P, 4, P], F32, name="factor_rows")
-        factor = keep.tile([P, 4, E], F32, name="factor")
-        y_codes = keep.tile([P, E * S], U32, name="y_codes", align_bytes=256)
-        y_scales = keep.tile([P, S], U8, name="y_scales", align_bytes=256)
+        factor_rows = keep.tile([P, SLOTS, P], F32, name="factor_rows")
+        factor = keep.tile([P, SLOTS, E], F32, name="factor")
+        y_codes = keep.tile([P, E * S], U32, name="y_codes", align_bytes=ALIGN)
+        y_scales = keep.tile([P, S], U8, name="y_scales", align_bytes=ALIGN)
 
-        raw, flat, windows, grouped = {}, {}, {}, {}
+        raw, windows, turned = {}, {}, {}
         x_codes, x_scales, a_codes, a_scales, y32, y16 = {}, {}, {}, {}, {}, {}
+        free_banks, bank_tiles = list(range(BANKS)), []
 
-        free, made = list(range(8)), [0]
-
-        def take(count):
-            chosen = free[:count][::-1]
-            free[:] = free[count:] + chosen
-            tiles = []
+        def take_banks(count):
+            chosen = free_banks[:count][::-1]
+            free_banks[:] = free_banks[count:] + chosen
             for place in chosen:
-                made[0] += 1
-                tiles.append(psum.tile([P, S], F32, name="bank%d" % made[0], offset=2048 * place))
-            return tiles
+                name = "bank%d" % len(bank_tiles)
+                bank_tiles.append(psum.tile([P, S], F32, name=name, offset=BANK_BYTES * place))
+            return bank_tiles[-count:]
+
+        def pair_rows(s, start):
+            return raw[s][:, start : start + 2 * ROW].rearrange("p (j k) -> p j k", j=2)
 
         def load(s):
-            kind, e, first, count = units[s]
+            kind, e, first, count = loads[s]
             if kind == "x":
                 src = x[e, P * first : P * (first + count), :].rearrange("(j p) k -> p j k", p=P)
             else:
-                src = a_down[e].rearrange("(p t) k -> p t k", t=4)[:, first : first + count, :]
+                src = a_down[e].rearrange("(p t) k -> p t k", t=SLOTS)[:, first : first + count, :]
             if count == 1:
-                raw[s] = work.tile([P, D], BF16, name="lone", bufs=SINGLE, align_bytes=256)
+                raw[s] = work.tile([P, D], BF16, name="single", bufs=len(head), align_bytes=ALIGN)
                 nc.sync.dma_start(out=raw[s][:], in_=src[:, 0, :])
             else:
-                flat[s] = work.tile([P, 2 * ROW + FRONT], BF16, name="raw", bufs=RAW_BUFS, align_bytes=256)
-                raw[s] = flat[s][:, : 2 * ROW].rearrange("p (j k) -> p j k", j=2)
-                nc.sync.dma_start(out=raw[s][:, :, FRONT : FRONT + D], in_=src)
-
-        def sort_pair(s):
-            halves = raw[s][:, :, FRONT : FRONT + D].rearrange("p j (r b u i) -> p j b r u i", r=2, u=2, i=HALF)
-            rows = flat[s][:, FRONT - HALF : FRONT - HALF + 2 * ROW].rearrange("p (j k) -> p j k", j=2)
-            span = rows[:, :, : 2 * REACH]
-            dst = span.rearrange("p j (r c i) -> p j c r i", r=2, i=HALF)[:, :, 0:64:2, :, :]
-            nc.vector.tensor_copy(out=dst, in_=halves[:, :, :, ::-1, 1, :])
-            for j in range(2):
-                windows[s, j] = [
-                    raw[s][:, j, FRONT + D // 2 : FRONT + D].bitcast(F32),
-                    raw[s][:, j, FRONT - HALF : FRONT - HALF + D // 2].bitcast(F32),
-                ]
+                raw[s] = work.tile([P, 2 * ROW + FRONT], BF16, name="pair", bufs=PAIR_BUFS, align_bytes=ALIGN)
+                nc.sync.dma_start(out=pair_rows(s, 0)[:, :, FRONT:], in_=src)
 
         def sort_single(s):
-            side = work.tile([P, 2, D // 2], BF16, name="side", bufs=3, align_bytes=64)
+            side = work.tile([P, 2, D // 2], BF16, name="side", bufs=SIDE_BUFS, align_bytes=ALIGN)
             halves = raw[s][:].rearrange("p (b u i) -> p u b i", u=2, i=HALF)
             nc.vector.tensor_copy(out=side[:].rearrange("p u (b i) -> p u b i", i=HALF), in_=halves)
-            windows[s, 0] = [side[:, w, :].bitcast(F32) for w in range(2)]
+            windows[s, 0] = [side[:, u, :].bitcast(F32) for u in range(2)]
+
+        def sort_pair(s):
+            rows, early = pair_rows(s, 0)[:, :, FRONT:], pair_rows(s, FRONT - HALF)
+            halves = rows.rearrange("p j (r b u i) -> p j b r u i", r=2, u=2, i=HALF)
+            places = early[:, :, : 2 * REACH].rearrange("p j (r c i) -> p j c r i", r=2, i=HALF)
+            nc.vector.tensor_copy(out=places[:, :, 0 : D // 2 // HALF : 2], in_=halves[:, :, :, ::-1, 1, :])
+            for j in range(2):
+                windows[s, j] = [rows[:, j, D // 2 :].bitcast(F32), early[:, j, : D // 2].bitcast(F32)]
 
         def sort(s):
-            if s <= last and (s, 0) not in windows:
-                if units[s][3] == 1:
-                    sort_single(s)
-                else:
-                    sort_pair(s)
+            if loads[s][3] == 1:
+                sort_single(s)
+            else:
+                sort_pair(s)
 
         def by_pass(s):
-            return units[s][0] == "x" and units[s][3] == 2 and s != last
+            return loads[s][0] == "x" and loads[s][3] == 2 and s != last
 
-        def turn(s, first, count, tiles):
-            moves = []
-            for b in range(first, first + count):
-                bank = tiles[b][:].rearrange("p (n u r) -> p n u r", n=2, u=2)
-                items = [(0, b), (1, b)] if by_pass(s) else [(b // 2, 2 * (b % 2)), (b // 2, 2 * (b % 2) + 1)]
-                for n, (j, g) in enumerate(items):
-                    for u in range(2):
-                        nc.tensor.transpose(bank[:, n, u, :], windows[s, j][u][:, P * g : P * (g + 1)], ident[:])
-                grouped[s, b] = work.tile([P, 4 * 2 * P], BF16, name="grouped", bufs=GROUPED, align_bytes=64)
-                dst = grouped[s, b][:].bitcast(F32).rearrange("p (n r u) -> p n r u", n=2, u=2)
-                moves.append((dst, bank.rearrange("p n u r -> p n r u")))
-            return moves
+        def turn(s, b, bank):
+            bank = bank[:].rearrange("p (n u r) -> p n u r", n=2, u=2)
+            for n in range(2):
+                j, g = (n, b) if by_pass(s) else (b // 2, 2 * (b % 2) + n)
+                for u in range(2):
+                    nc.tensor.transpose(bank[:, n, u, :], windows[s, j][u][:, P * g : P * (g + 1)], ident[:])
+            turned[s, b] = work.tile([P, SLOTS * BANK_COLS], BF16, name="turned", bufs=TURNED_BUFS, align_bytes=ALIGN)
+            words = turned[s, b][:].bitcast(F32).rearrange("p (n r u) -> p n r u", n=2, u=2)
+            return dict(out=words, in_=bank.rearrange("p n u r -> p n r u"))
 
         def x_span(e, g, cols):
             if e != last_e:
                 return slice(S * g + cols.start, S * g + cols.stop)
-            if cols.start == 0:
-                return slice(256 * g, 256 * (g + 1))
-            first = 1024 + 4 * (cols.start - 256) + P * g
-            return slice(first, first + P)
+            width = cols.stop - cols.start
+            first = PASSES * cols.start + width * g
+            return slice(first, first + width)
 
         def quantise(s, b):
-            kind, e, first, count = units[s]
+            kind, e, first, count = loads[s]
             if kind == "x":
                 if first == 0 and b == 0:
-                    x_codes[e] = work.tile([P, PASSES * S], U32, name="x_codes", align_bytes=64)
-                    x_scales[e] = work.tile([P, PASSES * S], U8, name="x_scales", align_bytes=64)
+                    x_codes[e] = work.tile([P, PASSES * S], U32, name="x_codes", align_bytes=ALIGN)
+                    x_scales[e] = work.tile([P, PASSES * S], U8, name="x_scales", align_bytes=ALIGN)
                 codes, scales = x_codes[e], x_scales[e]
+                tokens = slice(P * first, P * (first + count))
                 if count == 1:
-                    spans = [slice(S * g + P * first, S * g + P * (first + 1)) for g in (2 * b, 2 * b + 1)]
+                    spans = [x_span(e, g, tokens) for g in (2 * b, 2 * b + 1)]
                 elif by_pass(s):
-                    spans = [x_span(e, b, slice(P * first, P * (first + 2)))]
+                    spans = [x_span(e, b, tokens)]
                 else:
-                    spans = [slice(1024 + 256 * b, 1280 + 256 * b)]
+                    start = PASSES * tokens.start + BANK_COLS * b
+                    spans = [slice(start, start + BANK_COLS)]
             else:
                 t = first + b // 2
                 if b % 2 == 0:
-                    a_codes[e, t] = work.tile([P, PASSES * P], U32, name="a_codes", bufs=6, align_bytes=64)
-                    a_scales[e, t] = work.tile([P, PASSES * P], U8, name="a_scales", bufs=6, align_bytes=64)
+                    a_codes[e, t] = work.tile([P, PASSES * P], U32, name="a_codes", bufs=A_BUFS, align_bytes=ALIGN)
+                    a_scales[e, t] = work.tile([P, PASSES * P], U8, name="a_scales", bufs=A_BUFS, align_bytes=ALIGN)
                 codes, scales = a_codes[e, t], a_scales[e, t]
-                spans = [slice(256 * (b % 2), 256 * (b % 2 + 1))]
-            width = 1024 // len(spans)
+                spans = [slice(BANK_COLS * (b % 2), BANK_COLS * (b % 2 + 1))]
+            width = SLOTS * BANK_COLS // len(spans)
             for n, span in enumerate(spans):
                 nc.vector.quantize_mx(
                     out=codes[:, span].bitcast(FP8X4),
                     scales=scales[:, span],
-                    in_=grouped[s, b][:, width * n : width * (n + 1)],
+                    in_=turned[s, b][:, width * n : width * (n + 1)],
                 )
 
         def multiply(e, ts, cols, bank):
+            order = list(range(PASSES)) if e == 1 else list(range(PASSES))[::-1]
             width = cols.stop - cols.start
             for n, t in enumerate(ts):
-                order = ORDER if e != FORWARD else (0, 1, 2, 3)
                 for g in order:
                     span = x_span(e, g, cols)
                     nc.tensor.matmul_mx(
@@ -208,28 +196,25 @@ def tile_lora_down_scaled_rank_planes_g2_kernel(tc, x, a_down, gain, alpha, out_
                         stop=(g == order[-1]),
                     )
             if e not in y32:
-                y32[e] = work.tile([P, 4, S], F32, name="y32", bufs=3, align_bytes=256)
+                y32[e] = work.tile([P, SLOTS, S], F32, name="y32", bufs=Y_BUFS, align_bytes=ALIGN)
             for n, t in enumerate(ts):
                 src = bank[:, width * n : width * (n + 1)]
-                if cols.start == 384 and t in TAIL_V:
-                    nc.vector.tensor_scalar(
-                        out=y32[e][:, t, cols], in0=src, scalar1=factor[:, t, e : e + 1], scalar2=None, op0=MULT
-                    )
-                else:
-                    nc.scalar.activation(out=y32[e][:, t, cols], in_=src, func=COPY, scale=factor[:, t, e : e + 1])
+                nc.scalar.activation(out=y32[e][:, t, cols], in_=src, func=COPY, scale=factor[:, t, e : e + 1])
 
         def round_y(e, cols):
             if cols.start == 0:
-                y16[e] = work.tile([P, S, 4], BF16, name="y16", align_bytes=64)
+                y16[e] = work.tile([P, S, SLOTS], BF16, name="y16", align_bytes=ALIGN)
             nc.vector.tensor_copy(
                 out=y16[e][:, cols, :].rearrange("p (c i) t -> p c t i", i=4),
                 in_=y32[e][:, :, cols].rearrange("p t (c i) -> p c t i", i=4),
             )
 
+        def round_quarter(e, n):
+            round_y(e, slice(P * n, P * (n + 1)))
+
         def quantise_y(e, cols):
-            span = slice(S * e + cols.start, S * e + cols.stop)
             nc.vector.quantize_mx(
-                out=y_codes[:, span].bitcast(FP8X4),
+                out=y_codes[:, S * e + cols.start : S * e + cols.stop].bitcast(FP8X4),
                 scales=y_scales[4 * e :, cols],
                 in_=y16[e][:, cols, :].rearrange("p s t -> p (s t)"),
             )
@@ -239,102 +224,113 @@ def tile_lora_down_scaled_rank_planes_g2_kernel(tc, x, a_down, gain, alpha, out_
             nc.sync.dma_start(out=words_out[:, span], in_=y_codes[:, span].bitcast(I32))
 
         def store_y(e, ts, cols):
-            rows = out_0[e].rearrange("(p t) s -> p t s", t=4)
+            rows = out_0[e].rearrange("(p t) s -> p t s", t=SLOTS)
             nc.sync.dma_start(out=rows[:, ts, cols], in_=y32[e][:, ts, cols])
 
-        def store_scales(engines):
-            for q in range(4):
-                engines[q].dma_start(
-                    out=out_2[0, 4 * q : 4 * q + 4, :].bitcast(I32).rearrange("r (e s) -> e r s", e=E),
-                    in_=y_scales[32 * q : 32 * q + 4 * E, :].bitcast(I32),
-                )
+        def finish_y(e):
+            quantise_y(e, whole)
+            store_words(e, whole)
 
-        for s in range(SINGLE + RAW_BUFS):
-            if s <= last:
-                load(s)
+        def run_products(products):
+            for n, (e, ts, cols) in enumerate(products):
+                if n % 2 == 0:
+                    banks = take_banks(min(2, len(products) - n))
+                multiply(e, ts, cols, banks[n % 2])
+                if e == last_e and cols == low:
+                    store_y(e, slice(ts[0], ts[-1] + 1), cols)
+                elif e == last_e and ts[-1] == SLOTS - 1:
+                    store_y(e, slice(0, SLOTS), cols)
+                if e == last_e and ts[-1] == SLOTS - 1:
+                    if cols == third:
+                        store_words(e, low)
+                    round_y(e, cols)
+                    quantise_y(e, cols)
+
+        for s in range(len(head) + PAIR_BUFS):
+            load(s)
         with nc.allow_non_contiguous_dma(reason="one alpha to a partition"):
             nc.scalar.dma_start(out=alpha_sb[:], in_=alpha.rearrange("(e o) -> e o", o=1))
         nc.scalar.dma_start(out=gain_sb[:], in_=gain)
         make_identity(nc, ident[:])
         nc.vector.memset(factor_rows[:], 0.0)
         nc.scalar.activation(out=alpha_over_rank[:], in_=alpha_sb[:], func=COPY, scale=1.0 / R)
-
-        def make_factor():
-            nc.vector.tensor_scalar(
-                out=factor_rows[0:E],
-                in0=gain_sb[:].rearrange("e (p t) -> e t p", t=4),
-                scalar1=alpha_over_rank[:],
-                scalar2=None,
-                op0=MULT,
-            )
-
-        def turn_factor():
-            factor_bank = take(1)[0][:].rearrange("p (t r) -> p t r", t=4)
-            for t in range(4):
-                nc.tensor.transpose(factor_bank[:, t, :], factor_rows[:, t, :], ident[:])
-            nc.scalar.copy(out=factor[:], in_=factor_bank[:, :, 0:E])
-
         sort(0)
 
-        s, unsorted = 0, 1
-        held, rounding, quantising = [], [], []
-        for r, (run, products, order) in enumerate(runs):
-            banks = [(s + n, b) for n, unit in enumerate(run) for b in range(2 * unit[3])]
-            s += len(run)
-            filled = []
-            for n, (a, b) in enumerate(banks):
-                if b == 0:
-                    tiles = take(2 * units[a][3])
-                for dst, src in turn(a, b, 1, tiles):
-                    if "e" in order and not filled:
-                        filled.append((dst, src))
-                    else:
-                        nc.scalar.copy(out=dst, in_=src)
-            if r == FACTOR_AT:
-                turn_factor()
-            for a in range(s - len(run), s):
-                if units[a][3] == 2 and a + RAW_BUFS <= last:
-                    load(a + RAW_BUFS)
-            if len(rounding) * ROUND_COLS == S:
-                store_y(rounding[0][0], slice(0, 4), whole)
-            for item in order:
-                if item == "e":
-                    nc.vector.tensor_copy(out=filled[0][0], in_=filled[0][1])
-                elif item == "f":
-                    make_factor()
-                elif item == "h":
-                    while held:
-                        quantise(*held.pop(0))
-                elif item == "q":
-                    quantise(*banks.pop(0))
-                elif item == "s":
-                    sort(unsorted)
-                    unsorted += 1
-                elif item == "r":
-                    e, cols = rounding.pop(0)
-                    round_y(e, cols)
-                    if not rounding:
-                        quantising.append(e)
+        for s, (run, products) in enumerate(head):
+            for b, bank in enumerate(take_banks(2)):
+                nc.scalar.copy(**turn(s, b, bank))
+            if s == 2:
+                factor_bank = take_banks(1)[0][:].rearrange("p (t r) -> p t r", t=SLOTS)
+                for t in range(SLOTS):
+                    nc.tensor.transpose(factor_bank[:, t, :], factor_rows[:, t, :], ident[:])
+                nc.scalar.copy(out=factor[:], in_=factor_bank[:, :, 0:E])
+            if s + 1 < len(head):
+                sort(s + 1)
+            if s == 0:
+                nc.vector.tensor_scalar(
+                    out=factor_rows[0:E],
+                    in0=gain_sb[:].rearrange("e (p t) -> e t p", t=SLOTS),
+                    scalar1=alpha_over_rank[:],
+                    scalar2=None,
+                    op0=MULT,
+                )
+            else:
+                quantise(s - 1, 0)
+                quantise(s - 1, 1)
+            if s + 1 == len(head):
+                sort(s + 1)
+                quantise(s, 0)
+                quantise(s, 1)
+                sort(s + 2)
+            run_products(products)
+
+        for r, (run, products) in enumerate(body):
+            s = len(head) + 2 * r
+            banks = [(s + n, b) for n in range(2) for b in range(4)]
+            moves = []
+            for n in range(2):
+                for b, bank in enumerate(take_banks(4)):
+                    moves.append(turn(s + n, b, bank))
+                    if len(moves) > 1:
+                        nc.scalar.copy(**moves[-1])
+            for done in (s, s + 1):
+                if done + PAIR_BUFS <= last:
+                    load(done + PAIR_BUFS)
+            before = r // 2
+            if r % 2 == 0:
+                nc.vector.tensor_copy(**moves[0])
+                if before > 0:
+                    finish_y(before - 1)
+                for n, item in enumerate(banks[:-1]):
+                    if n == EARLY_SORT:
+                        sort(s + 2)
+                    quantise(*item)
+                sort(s + 3)
+            else:
+                store_y(before, slice(0, SLOTS), whole)
+                nc.vector.tensor_copy(**moves[0])
+                quantise(s - 1, 3)
+                for n in range(2):
+                    quantise(*banks[2 * n])
+                    quantise(*banks[2 * n + 1])
+                    round_quarter(before, n)
+                if s + 2 <= last:
+                    sort(s + 2)
+                round_quarter(before, 2)
+                round_quarter(before, 3)
+                quantise(*banks[4])
+                quantise(*banks[5])
+                if s + 3 <= last:
+                    sort(s + 3)
                 else:
-                    e = quantising.pop(0)
-                    quantise_y(e, whole)
-                    store_words(e, whole)
-            held += banks
-            for n, (e, ts, cols) in enumerate(products):
-                if n % PGROUP == 0:
-                    tiles = take(min(PGROUP, len(products) - n))
-                multiply(e, ts, cols, tiles[n % PGROUP])
-                if e == last_e:
-                    if cols.start == 0:
-                        store_y(e, slice(ts[0], ts[-1] + 1), cols)
-                    elif ts[-1] == 3:
-                        store_y(e, slice(0, 4), cols)
-                    if ts[-1] == 3:
-                        if cols.start == 256:
-                            store_words(e, first_half)
-                        round_y(e, cols)
-                        quantise_y(e, cols)
-                elif n == len(products) - 1 and ts[0] >= 2 and (e > 0 or ts[0] == 3):
-                    rounding = [(e, slice(c, c + ROUND_COLS)) for c in range(0, S, ROUND_COLS)]
-        store_words(last_e, second_half)
-        store_scales([nc.scalar, nc.scalar, nc.sync, nc.sync])
+                    finish_y(before)
+                quantise(*banks[6])
+                quantise(*banks[7])
+            run_products(products)
+
+        store_words(last_e, high)
+        for q, engine in enumerate((nc.scalar, nc.scalar, nc.sync, nc.sync)):
+            engine.dma_start(
+                out=out_2[0, 4 * q : 4 * q + 4, :].bitcast(I32).rearrange("r (e s) -> e r s", e=E),
+                in_=y_scales[32 * q : 32 * q + 4 * E, :].bitcast(I32),
+            )

@@ -22,11 +22,11 @@ BANKS = 8
 BANK_BYTES = 2048
 BANK_COLS = 256
 HALF = 16
-ALIGN = 256
+ALIGN = 512
 FRONT = ALIGN // 2
 ROW = FRONT + D
 REACH = D // 2 + 2 * HALF
-PAIR_BUFS = 10
+PAIR_BUFS = 9
 SIDE_BUFS = 3
 TURNED_BUFS = 10
 A_BUFS = 6

@@ -31,6 +31,7 @@ SIDE_BUFS = 3
 TURNED_BUFS = 10
 A_BUFS = 6
 Y_BUFS = 3
+WARM_UPS = 8
 EARLY_SORT = 2
 
 
@@ -77,7 +78,7 @@ def tile_lora_down_scaled_rank_planes_g2_kernel(tc, x, a_down, gain, alpha, out_
         gain_sb = keep.tile([E, R], BF16, name="gain_sb")
         alpha_sb = keep.tile([E, 1], BF16, name="alpha_sb")
         alpha_over_rank = keep.tile([E, 1], F32, name="alpha_over_rank")
-        factor_rows = keep.tile([P, SLOTS, P], F32, name="factor_rows")
+        factor_rows = keep.tile([P, SLOTS, P], F32, name="factor_rows", align_bytes=ALIGN)
         factor = keep.tile([P, SLOTS, E], F32, name="factor")
         y_codes = keep.tile([P, E * S], U32, name="y_codes", align_bytes=ALIGN)
         y_scales = keep.tile([P, S], U8, name="y_scales", align_bytes=ALIGN)
@@ -254,6 +255,24 @@ def tile_lora_down_scaled_rank_planes_g2_kernel(tc, x, a_down, gain, alpha, out_
         make_identity(nc, ident[:])
         nc.vector.memset(factor_rows[:], 0.0)
         nc.scalar.activation(out=alpha_over_rank[:], in_=alpha_sb[:], func=COPY, scale=1.0 / R)
+        zero_codes = keep.tile([P, S // 2], U32, name="zero_codes", align_bytes=ALIGN)
+        zero_scales = keep.tile([P, S // 2], U8, name="zero_scales", align_bytes=ALIGN)
+        nc.vector.quantize_mx(
+            out=zero_codes[:].bitcast(FP8X4),
+            scales=zero_scales[:],
+            in_=factor_rows[:].rearrange("p t r -> p (t r)").bitcast(BF16),
+        )
+        warm_bank = take_banks(1)[0]
+        for n in range(WARM_UPS):
+            nc.tensor.matmul_mx(
+                out=warm_bank[:, : S // 2],
+                lhsT=zero_codes[:, :P].bitcast(FP8X4),
+                lhsT_scale=zero_scales[:, :P],
+                rhs=zero_codes[:].bitcast(FP8X4),
+                rhs_scale=zero_scales[:],
+                start=True,
+                stop=True,
+            )
         sort(0)
 
         for s, (run, products) in enumerate(head):

@@ -25,9 +25,7 @@ HALF = 16
 ALIGN = 512
 FRONT = ALIGN // 2
 ROW = FRONT + D
-REACH = D // 2 + 2 * HALF
 PAIR_BUFS = 9
-SIDE_BUFS = 3
 TURNED_BUFS = 10
 A_BUFS = 6
 Y_BUFS = 3
@@ -95,8 +93,9 @@ def tile_lora_down_scaled_rank_planes_g2_kernel(tc, x, a_down, gain, alpha, out_
                 bank_tiles.append(psum.tile([P, S], F32, name=name, offset=BANK_BYTES * place))
             return bank_tiles[-count:]
 
-        def pair_rows(s, start):
-            return raw[s][:, start : start + 2 * ROW].rearrange("p (j k) -> p j k", j=2)
+        def chains(s, start):
+            pitch = FRONT + loads[s][3] * D // 2
+            return raw[s][:, start : start + 2 * pitch].rearrange("p (j k) -> p j k", j=2)
 
         def load(s):
             kind, e, first, count = loads[s]
@@ -105,31 +104,20 @@ def tile_lora_down_scaled_rank_planes_g2_kernel(tc, x, a_down, gain, alpha, out_
             else:
                 src = a_down[e].rearrange("(p t) k -> p t k", t=SLOTS)[:, first : first + count, :]
             if count == 1:
-                raw[s] = work.tile([P, D], BF16, name="single", bufs=len(head), align_bytes=ALIGN)
-                nc.sync.dma_start(out=raw[s][:], in_=src[:, 0, :])
+                raw[s] = work.tile([P, D + 3 * FRONT], BF16, name="single", bufs=len(head), align_bytes=ALIGN)
+                nc.sync.dma_start(out=chains(s, 0)[:, :, FRONT:], in_=src[:, 0, :].rearrange("p (h k) -> p h k", h=2))
             else:
                 raw[s] = work.tile([P, 2 * ROW + FRONT], BF16, name="pair", bufs=PAIR_BUFS, align_bytes=ALIGN)
-                nc.sync.dma_start(out=pair_rows(s, 0)[:, :, FRONT:], in_=src)
-
-        def sort_single(s):
-            side = work.tile([P, 2, D // 2], BF16, name="side", bufs=SIDE_BUFS, align_bytes=ALIGN)
-            halves = raw[s][:].rearrange("p (b u i) -> p u b i", u=2, i=HALF)
-            nc.vector.tensor_copy(out=side[:].rearrange("p u (b i) -> p u b i", i=HALF), in_=halves)
-            windows[s, 0] = [side[:, u, :].bitcast(F32) for u in range(2)]
-
-        def sort_pair(s):
-            rows, early = pair_rows(s, 0)[:, :, FRONT:], pair_rows(s, FRONT - HALF)
-            halves = rows.rearrange("p j (r b u i) -> p j b r u i", r=2, u=2, i=HALF)
-            places = early[:, :, : 2 * REACH].rearrange("p j (r c i) -> p j c r i", r=2, i=HALF)
-            nc.vector.tensor_copy(out=places[:, :, 0 : D // 2 // HALF : 2], in_=halves[:, :, :, ::-1, 1, :])
-            for j in range(2):
-                windows[s, j] = [rows[:, j, D // 2 :].bitcast(F32), early[:, j, : D // 2].bitcast(F32)]
+                nc.sync.dma_start(out=chains(s, 0)[:, :, FRONT:], in_=src)
 
         def sort(s):
-            if loads[s][3] == 1:
-                sort_single(s)
-            else:
-                sort_pair(s)
+            middle = loads[s][3] * D // 4
+            rows, early = chains(s, 0)[:, :, FRONT:], chains(s, FRONT - HALF)
+            halves = rows.rearrange("p j (r b u i) -> p j b r u i", r=2, u=2, i=HALF)
+            places = early[:, :, : 2 * (middle + 2 * HALF)].rearrange("p j (r c i) -> p j c r i", r=2, i=HALF)
+            nc.vector.tensor_copy(out=places[:, :, 0 : middle // HALF : 2], in_=halves[:, :, :, ::-1, 1, :])
+            for j in range(2):
+                windows[s, j] = [rows[:, j, middle:].bitcast(F32), early[:, j, :middle].bitcast(F32)]
 
         def by_pass(s):
             return loads[s][0] == "x" and loads[s][3] == 2 and s != last
@@ -137,7 +125,10 @@ def tile_lora_down_scaled_rank_planes_g2_kernel(tc, x, a_down, gain, alpha, out_
         def turn(s, b, bank):
             bank = bank[:].rearrange("p (n u r) -> p n u r", n=2, u=2)
             for n in range(2):
-                j, g = (n, b) if by_pass(s) else (b // 2, 2 * (b % 2) + n)
+                if loads[s][3] == 1:
+                    j, g = b, n
+                else:
+                    j, g = (n, b) if by_pass(s) else (b // 2, 2 * (b % 2) + n)
                 for u in range(2):
                     nc.tensor.transpose(bank[:, n, u, :], windows[s, j][u][:, P * g : P * (g + 1)], ident[:])
             turned[s, b] = work.tile([P, SLOTS * BANK_COLS], BF16, name="turned", bufs=TURNED_BUFS, align_bytes=ALIGN)

@@ -42,16 +42,16 @@ def tile_lora_down_scaled_rank_planes_g2_kernel(tc, x, a_down, gain, alpha, out_
     head = [
         ([("a", 0, 0, 1)], []),
         ([("x", 0, 0, 1)], []),
-        ([("x", 0, 1, 1)], []),
         ([("a", 0, 1, 1)], []),
-        ([("x", 0, 2, 1)], [(0, (0,), low)]),
-        ([("x", 0, 3, 1)], [(0, (1,), low)]),
+        ([("x", 0, 1, 1)], []),
         ([("a", 0, 2, 1)], []),
-        ([("a", 0, 3, 1)], [(0, (0, 1), high), (0, (2,), whole)]),
+        ([("a", 0, 3, 1)], [(0, (0,), low)]),
+        ([("x", 0, 2, 1)], [(0, (1,), low)]),
+        ([("x", 0, 3, 1)], [(0, (2, 3), low)]),
     ]
     body = []
     for e in range(1, last_e):
-        left_over = [(e - 1, (t,), whole) for t in ((3,) if e == 1 else (3, 2))]
+        left_over = [(e - 1, (t,), whole) for t in (3, 2)] if e > 1 else [(0, (0, 1), high), (0, (2, 3), high)]
         body.append(([("x", e, 0, 2), ("x", e, 2, 2)], left_over))
         body.append(([("a", e, 0, 2), ("a", e, 2, 2)], [(e, (0,), whole), (e, (1,), whole)]))
     body.append(([("a", last_e, 0, 2), ("x", last_e, 0, 2)], [(last_e - 1, (t,), whole) for t in (3, 2)]))
@@ -287,14 +287,35 @@ def tile_lora_down_scaled_rank_planes_g2_kernel(tc, x, a_down, gain, alpha, out_
             else:
                 quantise(s - 1, 0)
                 quantise(s - 1, 1)
-            if s + 1 == len(head):
-                sort(s + 1)
-                quantise(s, 0)
-                quantise(s, 1)
-                sort(s + 2)
             run_products(products)
 
-        for r, (run, products) in enumerate(body):
+        s = len(head)
+        sort(s)
+        quantise(s - 1, 0)
+        quantise(s - 1, 1)
+        for n, product in enumerate(body[0][1]):
+            moves = []
+            for b, bank in enumerate(take_banks(4)):
+                moves.append(turn(s + n, b, bank))
+                if n == 0 or b > 0:
+                    nc.scalar.copy(**moves[-1])
+            load(s + n + PAIR_BUFS)
+            if n == 0:
+                sort(s + 1)
+                round_quarter(0, 0)
+                round_quarter(0, 1)
+                for b in range(3):
+                    quantise(s, b)
+            else:
+                nc.vector.tensor_copy(**moves[0])
+                sort(s + 2)
+                quantise(s, 3)
+                for b in range(3):
+                    quantise(s + 1, b)
+                sort(s + 3)
+            run_products([product])
+
+        for r, (run, products) in list(enumerate(body))[1:]:
             s = len(head) + 2 * r
             banks = [(s + n, b) for n in range(2) for b in range(4)]
             moves = []
@@ -323,11 +344,12 @@ def tile_lora_down_scaled_rank_planes_g2_kernel(tc, x, a_down, gain, alpha, out_
                 for n in range(2):
                     quantise(*banks[2 * n])
                     quantise(*banks[2 * n + 1])
-                    round_quarter(before, n)
+                    round_quarter(before, n + 2 if before == 0 else n)
                 if s + 2 <= last:
                     sort(s + 2)
-                round_quarter(before, 2)
-                round_quarter(before, 3)
+                if before > 0:
+                    round_quarter(before, 2)
+                    round_quarter(before, 3)
                 quantise(*banks[4])
                 quantise(*banks[5])
                 if s + 3 <= last:

@@ -25,6 +25,8 @@ HALF = 16
 ALIGN = 512
 FRONT = ALIGN // 2
 ROW = FRONT + D
+REACH = D // 2 + 2 * HALF
+SIDE_BUFS = 3
 PAIR_BUFS = 9
 TURNED_BUFS = 10
 A_BUFS = 6
@@ -93,9 +95,8 @@ def tile_lora_down_scaled_rank_planes_g2_kernel(tc, x, a_down, gain, alpha, out_
                 bank_tiles.append(psum.tile([P, S], F32, name=name, offset=BANK_BYTES * place))
             return bank_tiles[-count:]
 
-        def chains(s, start):
-            pitch = FRONT + loads[s][3] * D // 2
-            return raw[s][:, start : start + 2 * pitch].rearrange("p (j k) -> p j k", j=2)
+        def pair_rows(s, start):
+            return raw[s][:, start : start + 2 * ROW].rearrange("p (j k) -> p j k", j=2)
 
         def load(s):
             kind, e, first, count = loads[s]
@@ -104,20 +105,31 @@ def tile_lora_down_scaled_rank_planes_g2_kernel(tc, x, a_down, gain, alpha, out_
             else:
                 src = a_down[e].rearrange("(p t) k -> p t k", t=SLOTS)[:, first : first + count, :]
             if count == 1:
-                raw[s] = work.tile([P, D + 3 * FRONT], BF16, name="single", bufs=len(head), align_bytes=ALIGN)
-                nc.sync.dma_start(out=chains(s, 0)[:, :, FRONT:], in_=src[:, 0, :].rearrange("p (h k) -> p h k", h=2))
+                raw[s] = work.tile([P, D], BF16, name="single", bufs=len(head), align_bytes=ALIGN)
+                nc.sync.dma_start(out=raw[s][:], in_=src[:, 0, :])
             else:
                 raw[s] = work.tile([P, 2 * ROW + FRONT], BF16, name="pair", bufs=PAIR_BUFS, align_bytes=ALIGN)
-                nc.sync.dma_start(out=chains(s, 0)[:, :, FRONT:], in_=src)
+                nc.sync.dma_start(out=pair_rows(s, 0)[:, :, FRONT:], in_=src)
+
+        def sort_single(s):
+            side = work.tile([P, 2, D // 2], BF16, name="side", bufs=SIDE_BUFS, align_bytes=ALIGN)
+            halves = raw[s][:].rearrange("p (b u i) -> p u b i", u=2, i=HALF)
+            nc.vector.tensor_copy(out=side[:].rearrange("p u (b i) -> p u b i", i=HALF), in_=halves)
+            windows[s, 0] = [side[:, u, :].bitcast(F32) for u in range(2)]
+
+        def sort_pair(s):
+            rows, early = pair_rows(s, 0)[:, :, FRONT:], pair_rows(s, FRONT - HALF)
+            halves = rows.rearrange("p j (r b u i) -> p j b r u i", r=2, u=2, i=HALF)
+            places = early[:, :, : 2 * REACH].rearrange("p j (r c i) -> p j c r i", r=2, i=HALF)
+            nc.vector.tensor_copy(out=places[:, :, 0 : D // 2 // HALF : 2], in_=halves[:, :, :, ::-1, 1, :])
+            for j in range(2):
+                windows[s, j] = [rows[:, j, D // 2 :].bitcast(F32), early[:, j, : D // 2].bitcast(F32)]
 
         def sort(s):
-            middle = loads[s][3] * D // 4
-            rows, early = chains(s, 0)[:, :, FRONT:], chains(s, FRONT - HALF)
-            halves = rows.rearrange("p j (r b u i) -> p j b r u i", r=2, u=2, i=HALF)
-            places = early[:, :, : 2 * (middle + 2 * HALF)].rearrange("p j (r c i) -> p j c r i", r=2, i=HALF)
-            nc.vector.tensor_copy(out=places[:, :, 0 : middle // HALF : 2], in_=halves[:, :, :, ::-1, 1, :])
-            for j in range(2):
-                windows[s, j] = [rows[:, j, middle:].bitcast(F32), early[:, j, :middle].bitcast(F32)]
+            if loads[s][3] == 1:
+                sort_single(s)
+            else:
+                sort_pair(s)
 
         def by_pass(s):
             return loads[s][0] == "x" and loads[s][3] == 2 and s != last
@@ -125,10 +137,7 @@ def tile_lora_down_scaled_rank_planes_g2_kernel(tc, x, a_down, gain, alpha, out_
         def turn(s, b, bank):
             bank = bank[:].rearrange("p (n u r) -> p n u r", n=2, u=2)
             for n in range(2):
-                if loads[s][3] == 1:
-                    j, g = b, n
-                else:
-                    j, g = (n, b) if by_pass(s) else (b // 2, 2 * (b % 2) + n)
+                j, g = (n, b) if by_pass(s) else (b // 2, 2 * (b % 2) + n)
                 for u in range(2):
                     nc.tensor.transpose(bank[:, n, u, :], windows[s, j][u][:, P * g : P * (g + 1)], ident[:])
             turned[s, b] = work.tile([P, SLOTS * BANK_COLS], BF16, name="turned", bufs=TURNED_BUFS, align_bytes=ALIGN)
@@ -221,7 +230,8 @@ def tile_lora_down_scaled_rank_planes_g2_kernel(tc, x, a_down, gain, alpha, out_
 
         def finish_y(e):
             quantise_y(e, whole)
-            store_words(e, whole)
+            if e == 1:
+                store_words(0, slice(0, 2 * S))
 
         def run_products(products):
             for n, (e, ts, cols) in enumerate(products):
@@ -230,11 +240,13 @@ def tile_lora_down_scaled_rank_planes_g2_kernel(tc, x, a_down, gain, alpha, out_
                 multiply(e, ts, cols, banks[n % 2])
                 if e == last_e and cols == low:
                     store_y(e, slice(ts[0], ts[-1] + 1), cols)
-                elif e == last_e and ts[-1] == SLOTS - 1:
-                    store_y(e, slice(0, SLOTS), cols)
-                if e == last_e and ts[-1] == SLOTS - 1:
-                    if cols == third:
+                    if ts[0] == 0:
+                        store_words(e - 1, whole)
+                if e == last_e and cols == fourth and ts[0] % 2 == 1:
+                    store_y(e, slice(ts[0] - 1, ts[0] + 1), high)
+                    if ts[0] == 1:
                         store_words(e, low)
+                if e == last_e and ts[-1] == SLOTS - 1:
                     round_y(e, cols)
                     quantise_y(e, cols)
 

@@ -240,7 +240,7 @@ def tile_lora_down_scaled_rank_planes_g2_kernel(tc, x, a_down, gain, alpha, out_
                 multiply(e, ts, cols, banks[n % 2])
                 if e == last_e and cols == low:
                     store_y(e, slice(ts[0], ts[-1] + 1), cols)
-                    if ts[0] == 0:
+                    if ts[0] == 2:
                         store_words(e - 1, whole)
                 if e == last_e and cols == fourth and ts[0] % 2 == 1:
                     store_y(e, slice(ts[0] - 1, ts[0] + 1), high)
@@ -342,8 +342,7 @@ def tile_lora_down_scaled_rank_planes_g2_kernel(tc, x, a_down, gain, alpha, out_
             before = r // 2
             if r % 2 == 0:
                 nc.vector.tensor_copy(**moves[0])
-                if before > 0:
-                    finish_y(before - 1)
+                finish_y(before - 1)
                 for n, item in enumerate(banks[:-1]):
                     if n == EARLY_SORT:
                         sort(s + 2)
@@ -359,7 +358,7 @@ def tile_lora_down_scaled_rank_planes_g2_kernel(tc, x, a_down, gain, alpha, out_
                     round_quarter(before, n + 2 if before == 0 else n)
                 if s + 2 <= last:
                     sort(s + 2)
-                if before > 0:
+                if before == 1:
                     round_quarter(before, 2)
                     round_quarter(before, 3)
                 quantise(*banks[4])
@@ -367,9 +366,12 @@ def tile_lora_down_scaled_rank_planes_g2_kernel(tc, x, a_down, gain, alpha, out_
                 if s + 3 <= last:
                     sort(s + 3)
                 else:
-                    finish_y(before)
+                    round_quarter(before, 2)
+                    round_quarter(before, 3)
                 quantise(*banks[6])
                 quantise(*banks[7])
+                if s + 3 > last:
+                    finish_y(before)
             run_products(products)
 
         store_words(last_e, high)

from contextlib import ExitStack

import concourse.mybir as mybir
from concourse.masks import make_identity

E, S, D, R = 4, 512, 2048, 512
FLOPS = 2 * E * S * D * R

F32 = mybir.dt.float32
BF16 = mybir.dt.bfloat16
U32 = mybir.dt.uint32
I32 = mybir.dt.int32
U8 = mybir.dt.uint8
FP8X4 = mybir.dt.float8_e4m3fn_x4
MULT = mybir.AluOpType.mult
COPY = mybir.ActivationFunctionType.Copy

P = 128
PASSES = D // 512
SLOTS = 4
BANKS = 8
BANK_BYTES = 2048
BANK_COLS = 256
HALF = 16
ALIGN = 512
FRONT = ALIGN // 2
ROW = FRONT + D
REACH = D // 2 + 2 * HALF
SIDE_BUFS = 3
PAIR_BUFS = 9
TURNED_BUFS = 10
A_BUFS = 6
Y_BUFS = 3
WARM_UPS = 8
EARLY_SORT = 2


def tile_lora_down_scaled_rank_planes_g2_kernel(tc, x, a_down, gain, alpha, out_0, out_1, out_2):
    nc = tc.nc
    last_e = E - 1
    whole, low, high = slice(0, S), slice(0, S // 2), slice(S // 2, S)
    third, fourth = slice(S // 2, S // 2 + P), slice(S // 2 + P, S)

    head = [
        ([("a", 0, 0, 1)], []),
        ([("x", 0, 0, 1)], []),
        ([("a", 0, 1, 1)], []),
        ([("x", 0, 1, 1)], []),
        ([("a", 0, 2, 1)], []),
        ([("a", 0, 3, 1)], [(0, (0,), low)]),
        ([("x", 0, 2, 1)], [(0, (1,), low)]),
        ([("x", 0, 3, 1)], [(0, (2, 3), low)]),
    ]
    body = []
    for e in range(1, last_e):
        left_over = [(e - 1, (t,), whole) for t in (3, 2)] if e > 1 else [(0, (0, 1), high), (0, (2, 3), high)]
        body.append(([("x", e, 0, 2), ("x", e, 2, 2)], left_over))
        body.append(([("a", e, 0, 2), ("a", e, 2, 2)], [(e, (0,), whole), (e, (1,), whole)]))
    body.append(([("a", last_e, 0, 2), ("x", last_e, 0, 2)], [(last_e - 1, (t,), whole) for t in (3, 2)]))
    body.append(
        (
            [("a", last_e, 2, 2), ("x", last_e, 2, 2)],
            [(last_e, ts, cols) for cols in (low, third) for ts in ((0, 1), (2, 3))]
            + [(last_e, (t,), fourth) for t in range(SLOTS)],
        )
    )
    loads = [item for run, products in head + body for item in run]
    last = len(loads) - 1
    words_out = out_1[0].rearrange("p m t -> p (m t)").bitcast(I32)

    with ExitStack() as ctx:
        keep = ctx.enter_context(tc.tile_pool(name="keep", bufs=1))
        work = ctx.enter_context(tc.tile_pool(name="work", bufs=2))
        psum = ctx.enter_context(tc.psum_pool(name="psum", bufs=1))
        ctx.enter_context(tc.manual_schedule())

        ident = keep.tile([P, P], F32, name="ident", align_bytes=ALIGN)
        gain_sb = keep.tile([E, R], BF16, name="gain_sb")
        alpha_sb = keep.tile([E, 1], BF16, name="alpha_sb")
        alpha_over_rank = keep.tile([E, 1], F32, name="alpha_over_rank")
        factor_rows = keep.tile([P, SLOTS, P], F32, name="factor_rows", align_bytes=ALIGN)
        factor = keep.tile([P, SLOTS, E], F32, name="factor")
        y_codes = keep.tile([P, E * S], U32, name="y_codes", align_bytes=ALIGN)
        y_scales = keep.tile([P, S], U8, name="y_scales", align_bytes=ALIGN)

        raw, windows, turned = {}, {}, {}
        x_codes, x_scales, a_codes, a_scales, y32, y16 = {}, {}, {}, {}, {}, {}
        free_banks, bank_tiles = list(range(BANKS)), []

        def take_banks(count):
            chosen = free_banks[:count][::-1]
            free_banks[:] = free_banks[count:] + chosen
            for place in chosen:
                name = "bank%d" % len(bank_tiles)
                bank_tiles.append(psum.tile([P, S], F32, name=name, offset=BANK_BYTES * place))
            return bank_tiles[-count:]

        def pair_rows(s, start):
            return raw[s][:, start : start + 2 * ROW].rearrange("p (j k) -> p j k", j=2)

        def load(s):
            kind, e, first, count = loads[s]
            if kind == "x":
                src = x[e, P * first : P * (first + count), :].rearrange("(j p) k -> p j k", p=P)
            else:
                src = a_down[e].rearrange("(p t) k -> p t k", t=SLOTS)[:, first : first + count, :]
            if count == 1:
                raw[s] = work.tile([P, D], BF16, name="single", bufs=len(head), align_bytes=ALIGN)
                nc.sync.dma_start(out=raw[s][:], in_=src[:, 0, :])
            else:
                raw[s] = work.tile([P, 2 * ROW + FRONT], BF16, name="pair", bufs=PAIR_BUFS, align_bytes=ALIGN)
                nc.sync.dma_start(out=pair_rows(s, 0)[:, :, FRONT:], in_=src)

        def sort_single(s):
            side = work.tile([P, 2, D // 2], BF16, name="side", bufs=SIDE_BUFS, align_bytes=ALIGN)
            halves = raw[s][:].rearrange("p (b u i) -> p u b i", u=2, i=HALF)
            nc.vector.tensor_copy(out=side[:].rearrange("p u (b i) -> p u b i", i=HALF), in_=halves)
            windows[s, 0] = [side[:, u, :].bitcast(F32) for u in range(2)]

        def sort_pair(s):
            rows, early = pair_rows(s, 0)[:, :, FRONT:], pair_rows(s, FRONT - HALF)
            halves = rows.rearrange("p j (r b u i) -> p j b r u i", r=2, u=2, i=HALF)
            places = early[:, :, : 2 * REACH].rearrange("p j (r c i) -> p j c r i", r=2, i=HALF)
            nc.vector.tensor_copy(out=places[:, :, 0 : D // 2 // HALF : 2], in_=halves[:, :, :, ::-1, 1, :])
            for j in range(2):
                windows[s, j] = [rows[:, j, D // 2 :].bitcast(F32), early[:, j, : D // 2].bitcast(F32)]

        def sort(s):
            if loads[s][3] == 1:
                sort_single(s)
            else:
                sort_pair(s)

        def by_pass(s):
            return loads[s][0] == "x" and loads[s][3] == 2 and s != last

        def turn(s, b, bank):
            bank = bank[:].rearrange("p (n u r) -> p n u r", n=2, u=2)
            for n in range(2):
                j, g = (n, b) if by_pass(s) else (b // 2, 2 * (b % 2) + n)
                for u in range(2):
                    nc.tensor.transpose(bank[:, n, u, :], windows[s, j][u][:, P * g : P * (g + 1)], ident[:])
            turned[s, b] = work.tile([P, SLOTS * BANK_COLS], BF16, name="turned", bufs=TURNED_BUFS, align_bytes=ALIGN)
            words = turned[s, b][:].bitcast(F32).rearrange("p (n r u) -> p n r u", n=2, u=2)
            return dict(out=words, in_=bank.rearrange("p n u r -> p n r u"))

        def x_span(e, g, cols):
            if e != last_e:
                return slice(S * g + cols.start, S * g + cols.stop)
            width = cols.stop - cols.start
            first = PASSES * cols.start + width * g
            return slice(first, first + width)

        def quantise(s, b):
            kind, e, first, count = loads[s]
            if kind == "x":
                if first == 0 and b == 0:
                    x_codes[e] = work.tile([P, PASSES * S], U32, name="x_codes", align_bytes=ALIGN)
                    x_scales[e] = work.tile([P, PASSES * S], U8, name="x_scales", align_bytes=ALIGN)
                codes, scales = x_codes[e], x_scales[e]
                tokens = slice(P * first, P * (first + count))
                if count == 1:
                    spans = [x_span(e, g, tokens) for g in (2 * b, 2 * b + 1)]
                elif by_pass(s):
                    spans = [x_span(e, b, tokens)]
                else:
                    start = PASSES * tokens.start + BANK_COLS * b
                    spans = [slice(start, start + BANK_COLS)]
            else:
                t = first + b // 2
                if b % 2 == 0:
                    a_codes[e, t] = work.tile([P, PASSES * P], U32, name="a_codes", bufs=A_BUFS, align_bytes=ALIGN)
                    a_scales[e, t] = work.tile([P, PASSES * P], U8, name="a_scales", bufs=A_BUFS, align_bytes=ALIGN)
                codes, scales = a_codes[e, t], a_scales[e, t]
                spans = [slice(BANK_COLS * (b % 2), BANK_COLS * (b % 2 + 1))]
            width = SLOTS * BANK_COLS // len(spans)
            for n, span in enumerate(spans):
                nc.vector.quantize_mx(
                    out=codes[:, span].bitcast(FP8X4),
                    scales=scales[:, span],
                    in_=turned[s, b][:, width * n : width * (n + 1)],
                )

        def multiply(e, ts, cols, bank):
            order = list(range(PASSES)) if e == 1 else list(range(PASSES))[::-1]
            width = cols.stop - cols.start
            for n, t in enumerate(ts):
                for g in order:
                    span = x_span(e, g, cols)
                    nc.tensor.matmul_mx(
                        out=bank[:, width * n : width * (n + 1)],
                        lhsT=a_codes[e, t][:, P * g : P * (g + 1)].bitcast(FP8X4),
                        lhsT_scale=a_scales[e, t][:, P * g : P * (g + 1)],
                        rhs=x_codes[e][:, span].bitcast(FP8X4),
                        rhs_scale=x_scales[e][:, span],
                        start=(g == order[0]),
                        stop=(g == order[-1]),
                    )
            if e not in y32:
                y32[e] = work.tile([P, SLOTS, S], F32, name="y32", bufs=Y_BUFS, align_bytes=ALIGN)
            for n, t in enumerate(ts):
                src = bank[:, width * n : width * (n + 1)]
                nc.scalar.activation(out=y32[e][:, t, cols], in_=src, func=COPY, scale=factor[:, t, e : e + 1])

        def round_y(e, cols):
            if cols.start == 0:
                y16[e] = work.tile([P, S, SLOTS], BF16, name="y16", align_bytes=ALIGN)
            nc.vector.tensor_copy(
                out=y16[e][:, cols, :].rearrange("p (c i) t -> p c t i", i=4),
                in_=y32[e][:, :, cols].rearrange("p t (c i) -> p c t i", i=4),
            )

        def round_quarter(e, n):
            round_y(e, slice(P * n, P * (n + 1)))

        def quantise_y(e, cols):
            nc.vector.quantize_mx(
                out=y_codes[:, S * e + cols.start : S * e + cols.stop].bitcast(FP8X4),
                scales=y_scales[4 * e :, cols],
                in_=y16[e][:, cols, :].rearrange("p s t -> p (s t)"),
            )

        def store_words(e, cols):
            span = slice(S * e + cols.start, S * e + cols.stop)
            nc.sync.dma_start(out=words_out[:, span], in_=y_codes[:, span].bitcast(I32))

        def store_y(e, ts, cols):
            rows = out_0[e].rearrange("(p t) s -> p t s", t=SLOTS)
            nc.sync.dma_start(out=rows[:, ts, cols], in_=y32[e][:, ts, cols])

        def finish_y(e):
            quantise_y(e, whole)
            if e == 1:
                store_words(0, slice(0, 2 * S))

        def run_products(products):
            for n, (e, ts, cols) in enumerate(products):
                if n % 2 == 0:
                    banks = take_banks(min(2, len(products) - n))
                multiply(e, ts, cols, banks[n % 2])
                if e == last_e and cols == low:
                    store_y(e, slice(ts[0], ts[-1] + 1), cols)
                    if ts[0] == 2:
                        store_words(e - 1, whole)
                if e == last_e and cols == fourth and ts[0] % 2 == 1:
                    store_y(e, slice(ts[0] - 1, ts[0] + 1), high)
                    if ts[0] == 1:
                        store_words(e, low)
                if e == last_e and ts[-1] == SLOTS - 1:
                    round_y(e, cols)
                    quantise_y(e, cols)

        for s in range(len(head) + PAIR_BUFS):
            load(s)
        with nc.allow_non_contiguous_dma(reason="one alpha to a partition"):
            nc.scalar.dma_start(out=alpha_sb[:], in_=alpha.rearrange("(e o) -> e o", o=1))
        nc.scalar.dma_start(out=gain_sb[:], in_=gain)
        make_identity(nc, ident[:])
        nc.vector.memset(factor_rows[:], 0.0)
        nc.scalar.activation(out=alpha_over_rank[:], in_=alpha_sb[:], func=COPY, scale=1.0 / R)
        zero_codes = keep.tile([P, S // 2], U32, name="zero_codes", align_bytes=ALIGN)
        zero_scales = keep.tile([P, S // 2], U8, name="zero_scales", align_bytes=ALIGN)
        nc.vector.quantize_mx(
            out=zero_codes[:].bitcast(FP8X4),
            scales=zero_scales[:],
            in_=factor_rows[:].rearrange("p t r -> p (t r)").bitcast(BF16),
        )
        warm_bank = take_banks(1)[0]
        for n in range(WARM_UPS):
            nc.tensor.matmul_mx(
                out=warm_bank[:, : S // 2],
                lhsT=zero_codes[:, :P].bitcast(FP8X4),
                lhsT_scale=zero_scales[:, :P],
                rhs=zero_codes[:].bitcast(FP8X4),
                rhs_scale=zero_scales[:],
                start=True,
                stop=True,
            )
        sort(0)

        for s, (run, products) in enumerate(head):
            for b, bank in enumerate(take_banks(2)):
                nc.scalar.copy(**turn(s, b, bank))
            if s == 2:
                factor_bank = take_banks(1)[0][:].rearrange("p (t r) -> p t r", t=SLOTS)
                for t in range(SLOTS):
                    nc.tensor.transpose(factor_bank[:, t, :], factor_rows[:, t, :], ident[:])
                nc.scalar.copy(out=factor[:], in_=factor_bank[:, :, 0:E])
            if s + 1 < len(head):
                sort(s + 1)
            if s == 0:
                nc.vector.tensor_scalar(
                    out=factor_rows[0:E],
                    in0=gain_sb[:].rearrange("e (p t) -> e t p", t=SLOTS),
                    scalar1=alpha_over_rank[:],
                    scalar2=None,
                    op0=MULT,
                )
            else:
                quantise(s - 1, 0)
                quantise(s - 1, 1)
            run_products(products)

        s = len(head)
        sort(s)
        quantise(s - 1, 0)
        quantise(s - 1, 1)
        for n, product in enumerate(body[0][1]):
            moves = []
            for b, bank in enumerate(take_banks(4)):
                moves.append(turn(s + n, b, bank))
                if n == 0 or b > 0:
                    nc.scalar.copy(**moves[-1])
            load(s + n + PAIR_BUFS)
            if n == 0:
                sort(s + 1)
                round_quarter(0, 0)
                round_quarter(0, 1)
                for b in range(3):
                    quantise(s, b)
            else:
                nc.vector.tensor_copy(**moves[0])
                sort(s + 2)
                quantise(s, 3)
                for b in range(3):
                    quantise(s + 1, b)
                sort(s + 3)
            run_products([product])

        for r, (run, products) in list(enumerate(body))[1:]:
            s = len(head) + 2 * r
            banks = [(s + n, b) for n in range(2) for b in range(4)]
            moves = []
            for n in range(2):
                for b, bank in enumerate(take_banks(4)):
                    moves.append(turn(s + n, b, bank))
                    if len(moves) > 1:
                        nc.scalar.copy(**moves[-1])
            for done in (s, s + 1):
                if done + PAIR_BUFS <= last:
                    load(done + PAIR_BUFS)
            before = r // 2
            if r % 2 == 0:
                nc.vector.tensor_copy(**moves[0])
                finish_y(before - 1)
                for n, item in enumerate(banks[:-1]):
                    if n == EARLY_SORT:
                        sort(s + 2)
                    quantise(*item)
                sort(s + 3)
            else:
                store_y(before, slice(0, SLOTS), whole)
                nc.vector.tensor_copy(**moves[0])
                quantise(s - 1, 3)
                for n in range(2):
                    quantise(*banks[2 * n])
                    quantise(*banks[2 * n + 1])
                    round_quarter(before, n + 2 if before == 0 else n)
                if s + 2 <= last:
                    sort(s + 2)
                if before == 1:
                    round_quarter(before, 2)
                    round_quarter(before, 3)
                quantise(*banks[4])
                quantise(*banks[5])
                if s + 3 <= last:
                    sort(s + 3)
                else:
                    round_quarter(before, 2)
                    round_quarter(before, 3)
                quantise(*banks[6])
                quantise(*banks[7])
                if s + 3 > last:
                    finish_y(before)
            run_products(products)

        store_words(last_e, high)
        for q, engine in enumerate((nc.scalar, nc.scalar, nc.sync, nc.sync)):
            engine.dma_start(
                out=out_2[0, 4 * q : 4 * q + 4, :].bitcast(I32).rearrange("r (e s) -> e r s", e=E),
                in_=y_scales[32 * q : 32 * q + 4 * E, :].bitcast(I32),
            )
